import numpy as np
import ml_dtypes


def mxq(x, axis, fmt="e4m3"):
    dtype, down = {"e4m3": (ml_dtypes.float8_e4m3fn, 7), "e5m2": (ml_dtypes.float8_e5m2, 14)}[fmt]
    v = np.moveaxis(np.asarray(x, np.float32).astype(ml_dtypes.bfloat16).astype(np.float64), axis, -1)
    blocks = v.reshape(v.shape[:-1] + (-1, 32))
    amax = np.abs(blocks).max(-1, keepdims=True)
    byte = np.maximum(np.where(amax > 0, np.frexp(amax)[1] - 1 + 127, 0) - down, 1)
    scale = np.exp2(byte - 127.0)
    codes = (blocks / scale).astype(np.float32).astype(dtype).astype(np.float64)
    return np.moveaxis((codes * scale).reshape(v.shape), -1, axis)


WIDE = False


def mx_kscale(k):
    if not WIDE:
        return np.ones(k)
    levels = np.array([24, -24, 12, -12, 0])
    if k % 512:
        return np.exp2(np.random.permutation(np.resize(levels, k // 32))).repeat(32)
    a = np.empty((k // 512, 16))
    for p in range(k // 512):
        a[p, :8] = np.random.permutation(np.resize(levels, 8))
        for g in range(8):
            far = levels[np.abs(levels - a[p, g]) >= 10]
            a[p, g + 8] = far[np.random.randint(len(far))]
    return np.exp2(a.ravel()).repeat(32)


def f64(x):
    return np.asarray(x).astype(np.float64)


def striped(idx):
    return np.tile(idx.reshape(-1, 16).T, (8, 1)).astype(np.uint16)


def unstriped(offs):
    return offs[:16].T.reshape(-1).astype(np.int64)


E2M1 = np.array([0.0, 0.5, 1.0, 1.5, 2.0, 3.0, 4.0, 6.0, -0.0, -0.5, -1.0, -1.5, -2.0, -3.0, -4.0, -6.0])


def pack_weight(w, fmt):
    k, n = w.shape
    w = f64(np.asarray(w, np.float32).astype(ml_dtypes.bfloat16)).reshape(k // 32, 32, n)
    amax = np.abs(w).max(1)
    if fmt == "e4m3":
        byte = np.frexp(amax)[1] - 1 + 127 - 7
    else:
        mant, ex = np.frexp(amax / 6.0)
        byte = np.where(mant > 0.5, ex, ex - 1) + 127
    byte = np.clip(np.where(amax > 0, byte, 1), 1, 254)
    scaled = (w * np.exp2(127.0 - byte)[:, None, :]).reshape(k, n).astype(np.float32)
    by_word = np.ascontiguousarray(scaled.reshape(k // 512, 128, 4, n).transpose(0, 1, 3, 2))
    if fmt == "e4m3":
        words = by_word.astype(ml_dtypes.float8_e4m3fn).view(np.uint8)
    else:
        c = by_word.astype(ml_dtypes.float4_e2m1fn).view(np.uint8) & 0xF
        words = (c[..., 0::2] | (c[..., 1::2] << 4)).reshape(k // 512, 128, 2 * n)
    return np.ascontiguousarray(words), np.ascontiguousarray(byte.astype(np.uint8).reshape(k // 512, 16, n))


def unpack_weight(words, scales, fmt):
    g, _, n = scales.shape
    words = np.ascontiguousarray(words).reshape(g, 128, n, -1)
    if fmt == "e4m3":
        vals = words.view(ml_dtypes.float8_e4m3fn).astype(np.float64)
    else:
        nib = np.empty((g, 128, n, 4), np.uint8)
        nib[..., 0::2] = words & 0xF
        nib[..., 1::2] = words >> 4
        vals = E2M1[nib]
    vals = vals * np.repeat(np.exp2(scales.astype(np.float64) - 127.0), 8, axis=1)[..., None]
    return vals.transpose(0, 1, 3, 2).reshape(g * 512, n)


def sigm(f):
    return 1.0 / (1.0 + np.exp(-np.maximum(f, -700.0)))


K, N, T, J = 512, 512, 2048, 1024


def setup_inputs():
    n = np.random.standard_normal
    s = mx_kscale(K)[:, None]
    p_tab = pack_weight(n((K, T)) * s, "e4m3")
    p_wa = pack_weight(n((K, N)) / np.sqrt(2 * K) / s, "e2m1")
    p_wc = pack_weight(n((K, N)) / np.sqrt(K) / s, "e2m1")
    return {
        "tab_words": p_tab[0],
        "tab_scales": p_tab[1],
        "wa_words": p_wa[0],
        "wa_scales": p_wa[1],
        "wb": (n((K, N)) / np.sqrt(2 * K) / s).astype(np.float32),
        "wc_words": p_wc[0],
        "wc_scales": p_wc[1],
        "wgo": np.tile(np.random.uniform(0.5, 2.0, J), (128, 1)).astype(np.float32),
        "offs": striped(np.random.permutation(T)[:J]),
        "offs2": striped(np.random.permutation(T)[:J]),
    }


def reference(tab_words, tab_scales, wa_words, wa_scales, wb, wc_words, wc_scales, wgo, offs, offs2):
    idx = unstriped(offs)
    idx2 = unstriped(offs2)
    tab_ = unpack_weight(tab_words, tab_scales, "e4m3")[:, idx]
    tabb_ = unpack_weight(tab_words, tab_scales, "e4m3")[:, idx2]
    wa_ = unpack_weight(wa_words, wa_scales, "e2m1")
    wb_ = mxq(f64(wb), 0, "e4m3")
    za = wa_.T @ tabb_ + wb_.T @ tab_
    eta = sigm(za)
    wc_ = unpack_weight(wc_words, wc_scales, "e2m1")
    ms = wc_.T @ tab_
    out = np.zeros((N, T))
    out[:, idx2] = f64(wgo)[0] * (eta * ms)
    return out

@@ -1,0 +1,215 @@
+from contextlib import ExitStack
+
+import concourse.mybir as mybir
+from concourse.masks import make_identity
+
+K, N, T, J = 512, 512, 2048, 1024
+FLOPS = 3 * 2 * K * N * J
+
+F32 = mybir.dt.float32
+BF16 = mybir.dt.bfloat16
+I32 = mybir.dt.int32
+U32 = mybir.dt.uint32
+U16 = mybir.dt.uint16
+U8 = mybir.dt.uint8
+FP8X4 = mybir.dt.float8_e4m3fn_x4
+FP4X4 = mybir.dt.float4_e2m1fn_x4
+COPY = mybir.ActivationFunctionType.Copy
+SIGMOID = mybir.ActivationFunctionType.Sigmoid
+MULT = mybir.AluOpType.mult
+
+P = 128
+PACK = 4
+HALF = 512
+N_TILES = N // P
+J_TILES = J // P
+LIST_ROWS = 16
+BANKS = 3
+
+
+def tile_list_rgg_none_kernel(
+    tc, tab_words, tab_scales, wa_words, wa_scales, wb, wc_words, wc_scales, wgo, offs, offs2, out
+):
+    nc = tc.nc
+
+    with ExitStack() as ctx:
+        keep = ctx.enter_context(tc.tile_pool(name="keep", bufs=1))
+        psum = ctx.enter_context(tc.psum_pool(name="psum", bufs=1))
+        banks = [psum.tile([P, HALF], F32, name="bank%d" % b) for b in range(BANKS)]
+        used = []
+
+        def take_bank():
+            used.append(len(used) % BANKS)
+            return banks[used[-1]]
+
+        src_list = keep.tile([P, J // LIST_ROWS], U16, name="src_list")
+        dst_list = keep.tile([P, J // LIST_ROWS], U16, name="dst_list")
+        tab_s = keep.tile([P, T], U8, name="tab_s", align_bytes=64)
+        wb_cols = [(0, 256), (256, 512)]
+        wb_raw = {}
+        wb_bf = [keep.tile([P, 256 * PACK], BF16, name="wb_bf0", align_bytes=64)]
+        wb_w = keep.tile([P, N], U32, name="wb_w", align_bytes=64)
+        wb_s = keep.tile([P, N], U8, name="wb_s", align_bytes=64)
+        src_w = keep.tile([P, J], U32, name="src_w", align_bytes=64)
+        src_s = keep.tile([P, J], U8, name="src_s", align_bytes=64)
+        dst_w = keep.tile([P, J], U32, name="dst_w", align_bytes=64)
+        dst_s = [keep.tile([P, HALF], U8, name="dst_s0", align_bytes=64)]
+        ident = keep.tile([P, P], F32, name="ident")
+        wgo_cols = keep.tile([P, J_TILES], F32, name="wgo_cols")
+        msw_t = [keep.tile([P, N], F32, name="msw_t%d" % jt) for jt in range(J_TILES)]
+        msw = [keep.tile([P, J], F32, name="msw%d" % nt) for nt in range(N_TILES)]
+        eta = [keep.tile([P, J], F32, name="eta%d" % nt) for nt in range(N_TILES)]
+        pages = [keep.tile([P, T], F32, name="page0")]
+
+        def load_scale_rows(plane, rows):
+            for q in range(4):
+                nc.sync.dma_start(plane[32 * q : 32 * q + 4].bitcast(I32), rows[0, 4 * q : 4 * q + 4, :].bitcast(I32))
+
+        def load_wb(i):
+            a, b = wb_cols[i]
+            wb_raw[i] = keep.tile([P, PACK, b - a], F32, name="wb_raw", tag="stage")
+            nc.sync.dma_start(wb_raw[i][:], wb.rearrange("(p t) n -> p t n", t=PACK)[:, :, a:b])
+
+        def entries(lst, lo, hi):
+            return lst[:, lo // LIST_ROWS : hi // LIST_ROWS]
+
+        def gather(dst, table, lst, lo, hi):
+            nc.vector.tensor_copy(dst, table[:].indirect(entries(lst, lo, hi)))
+
+        def round_wb(i):
+            nc.scalar.copy(
+                wb_bf[i][:].rearrange("p (c i t) -> p c t i", i=4, t=PACK),
+                wb_raw[i][:].rearrange("p t (c i) -> p c t i", i=4),
+            )
+
+        def quantize_wb(i):
+            a, b = wb_cols[i]
+            nc.vector.quantize_mx(out=wb_w[:, a:b].bitcast(FP8X4), scales=wb_s[:, a:b], in_=wb_bf[i][:])
+
+        def message_t(jt):
+            cols = slice(jt * P, (jt + 1) * P)
+            acc = take_bank()
+            nc.tensor.matmul_mx(
+                out=acc[:],
+                lhsT=src_w[:, cols].bitcast(FP8X4),
+                lhsT_scale=src_s[:, cols],
+                rhs=wc_w[:].bitcast(FP4X4),
+                rhs_scale=wc_s,
+                start=True,
+                stop=True,
+            )
+            nc.scalar.activation(msw_t[jt][:], acc[:], COPY, scale=wgo_cols[:, jt : jt + 1])
+
+        def message_back(nt, h):
+            acc = take_bank()
+            for i in range(HALF // P):
+                jt = h * (HALF // P) + i
+                nc.tensor.transpose(acc[:, i * P : (i + 1) * P], msw_t[jt][:, nt * P : (nt + 1) * P], ident[:])
+            nc.scalar.copy(msw[nt][:, h * HALF : (h + 1) * HALF], acc[:])
+
+        def gate(nt, h):
+            cols = slice(h * HALF, (h + 1) * HALF)
+            chans = slice(nt * P, (nt + 1) * P)
+            acc = take_bank()
+            nc.tensor.matmul_mx(
+                out=acc[:],
+                lhsT=wa_w[:, 2 * nt * P : 2 * (nt + 1) * P].bitcast(FP4X4),
+                lhsT_scale=wa_s[:, chans],
+                rhs=dst_w[:, cols].bitcast(FP8X4),
+                rhs_scale=dst_s[h][:],
+                start=True,
+                stop=False,
+            )
+            nc.tensor.matmul_mx(
+                out=acc[:],
+                lhsT=wb_w[:, chans].bitcast(FP8X4),
+                lhsT_scale=wb_s[:, chans],
+                rhs=src_w[:, cols].bitcast(FP8X4),
+                rhs_scale=src_s[:, cols],
+                start=False,
+                stop=True,
+            )
+            nc.scalar.activation(eta[nt][:, cols], acc[:], SIGMOID)
+
+        def scatter(nt, lo, hi):
+            page = pages[nt % 3]
+            nc.vector.tensor_tensor(page[:].indirect(entries(dst_list, lo, hi)), eta[nt][:, lo:hi], msw[nt][:, lo:hi], MULT)
+
+        def store(nt):
+            nc.sync.dma_start(out[nt * P : (nt + 1) * P, :], pages[nt % 3][:])
+
+        nc.vector.memset(tab_s[:].bitcast(I32), 0)
+        with tc.tile_pool(name="early", bufs=1) as early:
+            warm = early.tile([P, 4096], F32, name="warm")
+            nc.vector.memset(warm[:, 0:8], 0.0)
+            nc.scalar.activation(warm[:, 8:16], warm[:, 0:8], SIGMOID)
+        make_identity(nc, ident[:])
+        nc.sync.dma_start(src_list[:], offs)
+        load_scale_rows(tab_s[:], tab_scales)
+        nc.sync.dma_start(dst_list[:], offs2)
+        load_wb(0)
+        nc.vector.memset(pages[0][:].bitcast(I32), 0)
+
+        late = ctx.enter_context(tc.tile_pool(name="late", bufs=1))
+        tab_w = late.tile([P, T], U32, name="tab_w", tag="wide", align_bytes=64)
+        wc_w = late.tile([P, 2 * N], U8, name="wc_w", tag="wc", align_bytes=64)
+        wa_w = late.tile([P, 2 * N], U8, name="wa_w", align_bytes=64)
+        w_s = late.tile([P, 2 * N], U8, name="w_s", align_bytes=64)
+        wgo_rows = late.tile([P, P], F32, name="wgo_rows", tag="narrow", align_bytes=64)
+        wc_s = w_s[:, 0:N]
+        wa_s = w_s[:, N : 2 * N]
+        nc.vector.memset(w_s[:].bitcast(I32), 0)
+        nc.vector.memset(wgo_rows[:], 0.0)
+        nc.sync.dma_start(tab_w[:].bitcast(I32), tab_words[0].rearrange("p t i -> p (t i)").bitcast(I32))
+        nc.sync.dma_start(wc_w[:].bitcast(I32), wc_words[0].bitcast(I32))
+        load_scale_rows(wc_s, wc_scales)
+        nc.sync.dma_start(wgo_rows[0:J_TILES, :], wgo[0, :].rearrange("(a b) -> a b", b=P))
+        nc.sync.dma_start(wa_w[:].bitcast(I32), wa_words[0].bitcast(I32))
+        load_scale_rows(wa_s, wa_scales)
+        round_wb(0)
+        load_wb(1)
+
+        wgo_acc = take_bank()
+        nc.tensor.transpose(wgo_acc[:, 0:P], wgo_rows[:], ident[:])
+        nc.scalar.copy(wgo_cols[:], wgo_acc[:, 0:J_TILES])
+
+        gather(src_s[:], tab_s, src_list, 0, J)
+        quantize_wb(0)
+        gather(dst_s[0][:], tab_s, dst_list, 0, HALF)
+        gather(src_w[:, 0:HALF], tab_w, src_list, 0, HALF)
+        gather(dst_w[:, 0:HALF], tab_w, dst_list, 0, HALF)
+        gather(src_w[:, HALF:J], tab_w, src_list, HALF, J)
+        for jt in range(4):
+            message_t(jt)
+        dst_s.append(late.tile([P, HALF], U8, name="dst_s1", tag="narrow", align_bytes=64))
+        gather(dst_s[1][:], tab_s, dst_list, HALF, J)
+        gather(dst_w[:, HALF:J], tab_w, dst_list, HALF, J)
+        page1 = late.tile([P, T], F32, name="page1", tag="wide", align_bytes=64)
+        pages.append(page1)
+        nc.gpsimd.memset(page1[:], 0.0)
+        gate(0, 0)
+        message_back(0, 0)
+        scatter(0, 0, HALF)
+        message_back(1, 0)
+        gate(1, 0)
+        scatter(1, 0, HALF)
+        for jt in range(4, 8):
+            message_t(jt)
+        for nt in range(2):
+            message_back(nt, 1)
+            gate(nt, 1)
+            scatter(nt, HALF, J)
+            store(nt)
+            if nt == 0:
+                wb_bf.append(late.tile([P, 256 * PACK], BF16, name="wb_bf1", tag="wc", align_bytes=64))
+                round_wb(1)
+                quantize_wb(1)
+                page2 = keep.tile([P, T], F32, name="page2", tag="stage")
+                pages.append(page2)
+                nc.gpsimd.memset(page2[:], 0.0)
+        for nt in range(2, N_TILES):
+            for h in range(2):
+                message_back(nt, h)
+                gate(nt, h)
+            scatter(nt, 0, J)
+            store(nt)

@@ -1,7 +1,6 @@
 from contextlib import ExitStack
 
 import concourse.mybir as mybir
-from concourse.masks import make_identity
 
 K, N, T, J = 512, 512, 2048, 1024
 FLOPS = 3 * 2 * K * N * J
@@ -47,19 +46,16 @@ def tile_list_rgg_none_kernel(
         tab_s = keep.tile([P, T], U8, name="tab_s", align_bytes=64)
         wb_cols = [(0, 256), (256, 512)]
         wb_raw = {}
-        wb_bf = [keep.tile([P, 256 * PACK], BF16, name="wb_bf0", align_bytes=64)]
+        wb_bf = [keep.tile([P, 256 * PACK], BF16, name="wb_bf0", tag="rounded", align_bytes=64)]
         wb_w = keep.tile([P, N], U32, name="wb_w", align_bytes=64)
         wb_s = keep.tile([P, N], U8, name="wb_s", align_bytes=64)
         src_w = keep.tile([P, J], U32, name="src_w", align_bytes=64)
-        src_s = keep.tile([P, J], U8, name="src_s", align_bytes=64)
         dst_w = keep.tile([P, J], U32, name="dst_w", align_bytes=64)
-        dst_s = [keep.tile([P, HALF], U8, name="dst_s0", align_bytes=64)]
         ident = keep.tile([P, P], F32, name="ident")
-        wgo_cols = keep.tile([P, J_TILES], F32, name="wgo_cols")
         msw_t = [keep.tile([P, N], F32, name="msw_t%d" % jt) for jt in range(J_TILES)]
         msw = [keep.tile([P, J], F32, name="msw%d" % nt) for nt in range(N_TILES)]
         eta = [keep.tile([P, J], F32, name="eta%d" % nt) for nt in range(N_TILES)]
-        pages = [keep.tile([P, T], F32, name="page0")]
+        pages = []
 
         def load_scale_rows(plane, rows):
             for q in range(4):
@@ -67,7 +63,7 @@ def tile_list_rgg_none_kernel(
 
         def load_wb(i):
             a, b = wb_cols[i]
-            wb_raw[i] = keep.tile([P, PACK, b - a], F32, name="wb_raw", tag="stage")
+            wb_raw[i] = (keep if i else late).tile([P, PACK, b - a], F32, name="wb_raw", tag="second" if i else "first")
             nc.sync.dma_start(wb_raw[i][:], wb.rearrange("(p t) n -> p t n", t=PACK)[:, :, a:b])
 
         def entries(lst, lo, hi):
@@ -136,52 +132,63 @@ def tile_list_rgg_none_kernel(
             nc.vector.tensor_tensor(page[:].indirect(entries(dst_list, lo, hi)), eta[nt][:, lo:hi], msw[nt][:, lo:hi], MULT)
 
         def store(nt):
-            nc.sync.dma_start(out[nt * P : (nt + 1) * P, :], pages[nt % 3][:])
+            rows = slice(nt * P, (nt + 1) * P)
+            if nt < N_TILES - 1:
+                nc.sync.dma_start(out[rows, :], pages[nt % 3][:])
+            else:
+                nc.sync.dma_start(out[rows, 0 : T // 2], pages[nt % 3][:, 0 : T // 2])
+                nc.scalar.dma_start(out[rows, T // 2 : T], pages[nt % 3][:, T // 2 : T])
 
-        nc.vector.memset(tab_s[:].bitcast(I32), 0)
+        nc.gpsimd.memset(tab_s[:].bitcast(I32), 0)
+        wgo_rows = keep.tile([P, P], F32, name="wgo_rows", tag="second")
+        nc.vector.memset(wgo_rows[:], 0.0)
         with tc.tile_pool(name="early", bufs=1) as early:
-            warm = early.tile([P, 4096], F32, name="warm")
-            nc.vector.memset(warm[:, 0:8], 0.0)
-            nc.scalar.activation(warm[:, 8:16], warm[:, 0:8], SIGMOID)
-        make_identity(nc, ident[:])
+            diag = early.tile([P, P], I32, name="diag")
+            nc.gpsimd.iota(diag[:], [[1, P]], base=0, channel_multiplier=-1)
+            nc.vector.tensor_scalar(ident[:], diag[:], 0.0, None, mybir.AluOpType.is_equal)
+        warm = keep.tile([P, 1], F32, name="warm")
+        nc.scalar.activation(warm[:], ident[:, 0:1], SIGMOID)
         nc.sync.dma_start(src_list[:], offs)
         load_scale_rows(tab_s[:], tab_scales)
         nc.sync.dma_start(dst_list[:], offs2)
-        load_wb(0)
-        nc.vector.memset(pages[0][:].bitcast(I32), 0)
+        nc.sync.dma_start(wgo_rows[0:J_TILES, :], wgo[0, :].rearrange("(a b) -> a b", b=P))
 
         late = ctx.enter_context(tc.tile_pool(name="late", bufs=1))
         tab_w = late.tile([P, T], U32, name="tab_w", tag="wide", align_bytes=64)
         wc_w = late.tile([P, 2 * N], U8, name="wc_w", tag="wc", align_bytes=64)
         wa_w = late.tile([P, 2 * N], U8, name="wa_w", align_bytes=64)
         w_s = late.tile([P, 2 * N], U8, name="w_s", align_bytes=64)
-        wgo_rows = late.tile([P, P], F32, name="wgo_rows", tag="narrow", align_bytes=64)
+        src_s = late.tile([P, J], U8, name="src_s", align_bytes=64)
+        dst_s = [late.tile([P, HALF], U8, name="dst_s0", align_bytes=64)]
         wc_s = w_s[:, 0:N]
         wa_s = w_s[:, N : 2 * N]
         nc.vector.memset(w_s[:].bitcast(I32), 0)
-        nc.vector.memset(wgo_rows[:], 0.0)
+        page0 = late.tile([P, T], F32, name="page0")
+        pages.append(page0)
+        nc.gpsimd.memset(page0[:], 0.0)
         nc.sync.dma_start(tab_w[:].bitcast(I32), tab_words[0].rearrange("p t i -> p (t i)").bitcast(I32))
         nc.sync.dma_start(wc_w[:].bitcast(I32), wc_words[0].bitcast(I32))
         load_scale_rows(wc_s, wc_scales)
-        nc.sync.dma_start(wgo_rows[0:J_TILES, :], wgo[0, :].rearrange("(a b) -> a b", b=P))
+        load_wb(0)
         nc.sync.dma_start(wa_w[:].bitcast(I32), wa_words[0].bitcast(I32))
         load_scale_rows(wa_s, wa_scales)
         round_wb(0)
-        load_wb(1)
+        wgo_cols = late.tile([P, J_TILES], F32, name="wgo_cols", tag="first")
 
         wgo_acc = take_bank()
         nc.tensor.transpose(wgo_acc[:, 0:P], wgo_rows[:], ident[:])
         nc.scalar.copy(wgo_cols[:], wgo_acc[:, 0:J_TILES])
+        load_wb(1)
 
         gather(src_s[:], tab_s, src_list, 0, J)
-        quantize_wb(0)
         gather(dst_s[0][:], tab_s, dst_list, 0, HALF)
         gather(src_w[:, 0:HALF], tab_w, src_list, 0, HALF)
         gather(dst_w[:, 0:HALF], tab_w, dst_list, 0, HALF)
         gather(src_w[:, HALF:J], tab_w, src_list, HALF, J)
+        quantize_wb(0)
         for jt in range(4):
             message_t(jt)
-        dst_s.append(late.tile([P, HALF], U8, name="dst_s1", tag="narrow", align_bytes=64))
+        dst_s.append(keep.tile([P, HALF], U8, name="dst_s1", tag="rounded", align_bytes=64))
         gather(dst_s[1][:], tab_s, dst_list, HALF, J)
         gather(dst_w[:, HALF:J], tab_w, dst_list, HALF, J)
         page1 = late.tile([P, T], F32, name="page1", tag="wide", align_bytes=64)
@@ -204,7 +211,7 @@ def tile_list_rgg_none_kernel(
                 wb_bf.append(late.tile([P, 256 * PACK], BF16, name="wb_bf1", tag="wc", align_bytes=64))
                 round_wb(1)
                 quantize_wb(1)
-                page2 = keep.tile([P, T], F32, name="page2", tag="stage")
+                page2 = keep.tile([P, T], F32, name="page2", tag="second")
                 pages.append(page2)
                 nc.gpsimd.memset(page2[:], 0.0)
         for nt in range(2, N_TILES):

@@ -46,11 +46,11 @@ def tile_list_rgg_none_kernel(
         tab_s = keep.tile([P, T], U8, name="tab_s", align_bytes=64)
         wb_cols = [(0, 256), (256, 512)]
         wb_raw = {}
-        wb_bf = [keep.tile([P, 256 * PACK], BF16, name="wb_bf0", tag="rounded", align_bytes=64)]
+        wb_bf = []
         wb_w = keep.tile([P, N], U32, name="wb_w", align_bytes=64)
         wb_s = keep.tile([P, N], U8, name="wb_s", align_bytes=64)
         src_w = keep.tile([P, J], U32, name="src_w", align_bytes=64)
-        dst_w = keep.tile([P, J], U32, name="dst_w", align_bytes=64)
+        dst_w = [keep.tile([P, HALF], U32, name="dst_w0", align_bytes=64)]
         ident = keep.tile([P, P], F32, name="ident")
         msw_t = [keep.tile([P, N], F32, name="msw_t%d" % jt) for jt in range(J_TILES)]
         msw = [keep.tile([P, J], F32, name="msw%d" % nt) for nt in range(N_TILES)]
@@ -111,7 +111,7 @@ def tile_list_rgg_none_kernel(
                 out=acc[:],
                 lhsT=wa_w[:, 2 * nt * P : 2 * (nt + 1) * P].bitcast(FP4X4),
                 lhsT_scale=wa_s[:, chans],
-                rhs=dst_w[:, cols].bitcast(FP8X4),
+                rhs=dst_w[h][:].bitcast(FP8X4),
                 rhs_scale=dst_s[h][:],
                 start=True,
                 stop=False,
@@ -165,37 +165,42 @@ def tile_list_rgg_none_kernel(
         nc.vector.memset(w_s[:].bitcast(I32), 0)
         page0 = late.tile([P, T], F32, name="page0")
         pages.append(page0)
-        nc.gpsimd.memset(page0[:], 0.0)
+        nc.vector.memset(page0[:].bitcast(I32), 0)
         nc.sync.dma_start(tab_w[:].bitcast(I32), tab_words[0].rearrange("p t i -> p (t i)").bitcast(I32))
         nc.sync.dma_start(wc_w[:].bitcast(I32), wc_words[0].bitcast(I32))
         load_scale_rows(wc_s, wc_scales)
         load_wb(0)
         nc.sync.dma_start(wa_w[:].bitcast(I32), wa_words[0].bitcast(I32))
         load_scale_rows(wa_s, wa_scales)
-        round_wb(0)
-        wgo_cols = late.tile([P, J_TILES], F32, name="wgo_cols", tag="first")
+        with tc.tile_pool(name="mid", bufs=1) as mid:
+            wb_bf.append(mid.tile([P, 256 * PACK], BF16, name="wb_bf0", align_bytes=64))
+            round_wb(0)
+            wgo_cols = late.tile([P, J_TILES], F32, name="wgo_cols", tag="first")
 
-        wgo_acc = take_bank()
-        nc.tensor.transpose(wgo_acc[:, 0:P], wgo_rows[:], ident[:])
-        nc.scalar.copy(wgo_cols[:], wgo_acc[:, 0:J_TILES])
-        load_wb(1)
+            wgo_acc = take_bank()
+            nc.tensor.transpose(wgo_acc[:, 0:P], wgo_rows[:], ident[:])
+            nc.scalar.copy(wgo_cols[:], wgo_acc[:, 0:J_TILES])
+            load_wb(1)
 
-        gather(src_s[:], tab_s, src_list, 0, J)
-        gather(dst_s[0][:], tab_s, dst_list, 0, HALF)
-        gather(src_w[:, 0:HALF], tab_w, src_list, 0, HALF)
-        gather(dst_w[:, 0:HALF], tab_w, dst_list, 0, HALF)
-        gather(src_w[:, HALF:J], tab_w, src_list, HALF, J)
-        quantize_wb(0)
+            gather(src_s[:], tab_s, src_list, 0, J)
+            gather(dst_s[0][:], tab_s, dst_list, 0, HALF)
+            gather(src_w[:, 0:256], tab_w, src_list, 0, 256)
+            gather(src_w[:, 256:HALF], tab_w, src_list, 256, HALF)
+            gather(dst_w[0][:], tab_w, dst_list, 0, HALF)
+            gather(src_w[:, HALF:J], tab_w, src_list, HALF, J)
+            quantize_wb(0)
+        last = ctx.enter_context(tc.tile_pool(name="last", bufs=1))
         for jt in range(4):
             message_t(jt)
-        dst_s.append(keep.tile([P, HALF], U8, name="dst_s1", tag="rounded", align_bytes=64))
+        dst_s.append(last.tile([P, HALF], U8, name="dst_s1", align_bytes=64))
+        dst_w.append(last.tile([P, HALF], U32, name="dst_w1", align_bytes=64))
         gather(dst_s[1][:], tab_s, dst_list, HALF, J)
-        gather(dst_w[:, HALF:J], tab_w, dst_list, HALF, J)
+        gather(dst_w[1][:], tab_w, dst_list, HALF, J)
         page1 = late.tile([P, T], F32, name="page1", tag="wide", align_bytes=64)
         pages.append(page1)
         nc.gpsimd.memset(page1[:], 0.0)
-        gate(0, 0)
         message_back(0, 0)
+        gate(0, 0)
         scatter(0, 0, HALF)
         message_back(1, 0)
         gate(1, 0)
@@ -211,7 +216,7 @@ def tile_list_rgg_none_kernel(
                 wb_bf.append(late.tile([P, 256 * PACK], BF16, name="wb_bf1", tag="wc", align_bytes=64))
                 round_wb(1)
                 quantize_wb(1)
-                page2 = keep.tile([P, T], F32, name="page2", tag="second")
+                page2 = late.tile([P, T], F32, name="page2", tag="wc", align_bytes=64)
                 pages.append(page2)
                 nc.gpsimd.memset(page2[:], 0.0)
         for nt in range(2, N_TILES):

@@ -1,6 +1,7 @@
 from contextlib import ExitStack
 
 import concourse.mybir as mybir
+from concourse.masks import make_identity
 
 K, N, T, J = 512, 512, 2048, 1024
 FLOPS = 3 * 2 * K * N * J
@@ -23,7 +24,7 @@ HALF = 512
 N_TILES = N // P
 J_TILES = J // P
 LIST_ROWS = 16
-BANKS = 3
+QUAD = 32
 
 
 def tile_list_rgg_none_kernel(
@@ -34,37 +35,50 @@ def tile_list_rgg_none_kernel(
     with ExitStack() as ctx:
         keep = ctx.enter_context(tc.tile_pool(name="keep", bufs=1))
         psum = ctx.enter_context(tc.psum_pool(name="psum", bufs=1))
-        banks = [psum.tile([P, HALF], F32, name="bank%d" % b) for b in range(BANKS)]
-        used = []
-
-        def take_bank():
-            used.append(len(used) % BANKS)
-            return banks[used[-1]]
+        bank_m = psum.tile([P, HALF], F32, name="bank_m")
+        bank_g = psum.tile([P, HALF], F32, name="bank_g")
+        bank_t = psum.tile([P, HALF], F32, name="bank_t")
 
         src_list = keep.tile([P, J // LIST_ROWS], U16, name="src_list")
         dst_list = keep.tile([P, J // LIST_ROWS], U16, name="dst_list")
         tab_s = keep.tile([P, T], U8, name="tab_s", align_bytes=64)
-        wb_cols = [(0, 256), (256, 512)]
-        wb_raw = {}
-        wb_bf = []
+        shared = ctx.enter_context(tc.tile_pool(name="shared", bufs=1))
+        tab_w = shared.tile([P, T], U32, name="tab_w", offset=4096, align_bytes=64)
+        wb_raw = [keep.tile([P, PACK, N // 2], F32, name="wb_raw%d" % i) for i in range(2)]
+        wb_bf = [shared.tile([P, 256 * PACK], BF16, name="wb_bf0", offset=16384 + 1536, align_bytes=64)]
         wb_w = keep.tile([P, N], U32, name="wb_w", align_bytes=64)
         wb_s = keep.tile([P, N], U8, name="wb_s", align_bytes=64)
-        src_w = keep.tile([P, J], U32, name="src_w", align_bytes=64)
+        wc_w = keep.tile([P, 2 * N], U8, name="wc_w", align_bytes=64)
+        wa_w = keep.tile([P, 2 * N], U8, name="wa_w", align_bytes=64)
+        w_s = keep.tile([P, 2 * N], U8, name="w_s", align_bytes=64)
+        wc_s = w_s[:, 0:N]
+        wa_s = w_s[:, N : 2 * N]
+        src_s = [keep.tile([P, HALF], U8, name="src_s0", align_bytes=64)]
+        dst_s = [keep.tile([P, HALF], U8, name="dst_s0", align_bytes=64)]
+        src_w = [keep.tile([P, HALF], U32, name="src_w0", align_bytes=64)]
         dst_w = [keep.tile([P, HALF], U32, name="dst_w0", align_bytes=64)]
         ident = keep.tile([P, P], F32, name="ident")
-        msw_t = [keep.tile([P, N], F32, name="msw_t%d" % jt) for jt in range(J_TILES)]
+        wgo_rows = keep.tile([P, P], F32, name="wgo_rows")
+        wgo_cols = keep.tile([P, J_TILES], F32, name="wgo_cols")
         msw = [keep.tile([P, J], F32, name="msw%d" % nt) for nt in range(N_TILES)]
         eta = [keep.tile([P, J], F32, name="eta%d" % nt) for nt in range(N_TILES)]
-        pages = []
+        warm = keep.tile([P, 1], F32, name="warm")
+        page0 = keep.tile([P, T], F32, name="page0")
+        pages = [page0]
 
         def load_scale_rows(plane, rows):
             for q in range(4):
-                nc.sync.dma_start(plane[32 * q : 32 * q + 4].bitcast(I32), rows[0, 4 * q : 4 * q + 4, :].bitcast(I32))
+                nc.sync.dma_start(plane[QUAD * q : QUAD * q + 4].bitcast(I32), rows[0, 4 * q : 4 * q + 4, :].bitcast(I32))
+
+        def load_table_scales():
+            for q in range(4):
+                rows = tab_scales[0, 4 * q : 4 * q + 4, :].bitcast(I32)
+                nc.sync.dma_start(
+                    tab_s[QUAD * q : QUAD * (q + 1)].bitcast(I32), rows.unsqueeze(0).to_broadcast([QUAD // 4, 4, T // 4])
+                )
 
         def load_wb(i):
-            a, b = wb_cols[i]
-            wb_raw[i] = (keep if i else late).tile([P, PACK, b - a], F32, name="wb_raw", tag="second" if i else "first")
-            nc.sync.dma_start(wb_raw[i][:], wb.rearrange("(p t) n -> p t n", t=PACK)[:, :, a:b])
+            nc.sync.dma_start(wb_raw[i][:], wb.rearrange("(p t) n -> p t n", t=PACK)[:, :, i * 256 : (i + 1) * 256])
 
         def entries(lst, lo, hi):
             return lst[:, lo // LIST_ROWS : hi // LIST_ROWS]
@@ -79,53 +93,50 @@ def tile_list_rgg_none_kernel(
             )
 
         def quantize_wb(i):
-            a, b = wb_cols[i]
-            nc.vector.quantize_mx(out=wb_w[:, a:b].bitcast(FP8X4), scales=wb_s[:, a:b], in_=wb_bf[i][:])
+            cols = slice(i * 256, (i + 1) * 256)
+            nc.vector.quantize_mx(out=wb_w[:, cols].bitcast(FP8X4), scales=wb_s[:, cols], in_=wb_bf[i][:])
 
-        def message_t(jt):
-            cols = slice(jt * P, (jt + 1) * P)
-            acc = take_bank()
-            nc.tensor.matmul_mx(
-                out=acc[:],
-                lhsT=src_w[:, cols].bitcast(FP8X4),
-                lhsT_scale=src_s[:, cols],
-                rhs=wc_w[:].bitcast(FP4X4),
-                rhs_scale=wc_s,
-                start=True,
-                stop=True,
-            )
-            nc.scalar.activation(msw_t[jt][:], acc[:], COPY, scale=wgo_cols[:, jt : jt + 1])
-
-        def message_back(nt, h):
-            acc = take_bank()
-            for i in range(HALF // P):
-                jt = h * (HALF // P) + i
-                nc.tensor.transpose(acc[:, i * P : (i + 1) * P], msw_t[jt][:, nt * P : (nt + 1) * P], ident[:])
-            nc.scalar.copy(msw[nt][:, h * HALF : (h + 1) * HALF], acc[:])
-
-        def gate(nt, h):
+        def half_tile(nt, h):
+            stage = keep.tile([P, HALF], F32, name="stage", tag="stage%d" % (nt % 2), align_bytes=64)
             cols = slice(h * HALF, (h + 1) * HALF)
             chans = slice(nt * P, (nt + 1) * P)
-            acc = take_bank()
+            for i in range(HALF // P):
+                nc.tensor.matmul_mx(
+                    out=bank_m[:, i * P : (i + 1) * P],
+                    lhsT=src_w[h][:, i * P : (i + 1) * P].bitcast(FP8X4),
+                    lhsT_scale=src_s[h][:, i * P : (i + 1) * P],
+                    rhs=wc_w[:, 2 * nt * P : 2 * (nt + 1) * P].bitcast(FP4X4),
+                    rhs_scale=wc_s[:, chans],
+                    start=True,
+                    stop=True,
+                )
+            for i in range(HALF // P):
+                jt = h * (HALF // P) + i
+                nc.scalar.activation(
+                    stage[:, i * P : (i + 1) * P], bank_m[:, i * P : (i + 1) * P], COPY, scale=wgo_cols[:, jt : jt + 1]
+                )
             nc.tensor.matmul_mx(
-                out=acc[:],
-                lhsT=wa_w[:, 2 * nt * P : 2 * (nt + 1) * P].bitcast(FP4X4),
-                lhsT_scale=wa_s[:, chans],
-                rhs=dst_w[h][:].bitcast(FP8X4),
-                rhs_scale=dst_s[h][:],
+                out=bank_g[:],
+                lhsT=wb_w[:, chans].bitcast(FP8X4),
+                lhsT_scale=wb_s[:, chans],
+                rhs=src_w[h][:].bitcast(FP8X4),
+                rhs_scale=src_s[h][:],
                 start=True,
                 stop=False,
             )
             nc.tensor.matmul_mx(
-                out=acc[:],
-                lhsT=wb_w[:, chans].bitcast(FP8X4),
-                lhsT_scale=wb_s[:, chans],
-                rhs=src_w[:, cols].bitcast(FP8X4),
-                rhs_scale=src_s[:, cols],
+                out=bank_g[:],
+                lhsT=wa_w[:, 2 * nt * P : 2 * (nt + 1) * P].bitcast(FP4X4),
+                lhsT_scale=wa_s[:, chans],
+                rhs=dst_w[h][:].bitcast(FP8X4),
+                rhs_scale=dst_s[h][:],
                 start=False,
                 stop=True,
             )
-            nc.scalar.activation(eta[nt][:, cols], acc[:], SIGMOID)
+            for i in range(HALF // P):
+                nc.tensor.transpose(bank_t[:, i * P : (i + 1) * P], stage[:, i * P : (i + 1) * P], ident[:])
+            nc.scalar.activation(eta[nt][:, cols], bank_g[:], SIGMOID)
+            nc.scalar.copy(msw[nt][:, cols], bank_t[:])
 
         def scatter(nt, lo, hi):
             page = pages[nt % 3]
@@ -139,89 +150,57 @@ def tile_list_rgg_none_kernel(
                 nc.sync.dma_start(out[rows, 0 : T // 2], pages[nt % 3][:, 0 : T // 2])
                 nc.scalar.dma_start(out[rows, T // 2 : T], pages[nt % 3][:, T // 2 : T])
 
-        nc.gpsimd.memset(tab_s[:].bitcast(I32), 0)
-        wgo_rows = keep.tile([P, P], F32, name="wgo_rows", tag="second")
-        nc.vector.memset(wgo_rows[:], 0.0)
-        with tc.tile_pool(name="early", bufs=1) as early:
-            diag = early.tile([P, P], I32, name="diag")
-            nc.gpsimd.iota(diag[:], [[1, P]], base=0, channel_multiplier=-1)
-            nc.vector.tensor_scalar(ident[:], diag[:], 0.0, None, mybir.AluOpType.is_equal)
-        warm = keep.tile([P, 1], F32, name="warm")
-        nc.scalar.activation(warm[:], ident[:, 0:1], SIGMOID)
-        nc.sync.dma_start(src_list[:], offs)
-        load_scale_rows(tab_s[:], tab_scales)
-        nc.sync.dma_start(dst_list[:], offs2)
-        nc.sync.dma_start(wgo_rows[0:J_TILES, :], wgo[0, :].rearrange("(a b) -> a b", b=P))
-
-        late = ctx.enter_context(tc.tile_pool(name="late", bufs=1))
-        tab_w = late.tile([P, T], U32, name="tab_w", tag="wide", align_bytes=64)
-        wc_w = late.tile([P, 2 * N], U8, name="wc_w", tag="wc", align_bytes=64)
-        wa_w = late.tile([P, 2 * N], U8, name="wa_w", align_bytes=64)
-        w_s = late.tile([P, 2 * N], U8, name="w_s", align_bytes=64)
-        src_s = late.tile([P, J], U8, name="src_s", align_bytes=64)
-        dst_s = [late.tile([P, HALF], U8, name="dst_s0", align_bytes=64)]
-        wc_s = w_s[:, 0:N]
-        wa_s = w_s[:, N : 2 * N]
         nc.vector.memset(w_s[:].bitcast(I32), 0)
-        page0 = late.tile([P, T], F32, name="page0")
-        pages.append(page0)
+        nc.vector.memset(wgo_rows[:], 0.0)
+        make_identity(nc, ident[:])
         nc.vector.memset(page0[:].bitcast(I32), 0)
+        nc.scalar.activation(warm[:], page0[:, 0:1], SIGMOID)
+
+        nc.sync.dma_start(src_list[:], offs)
+        load_table_scales()
+        nc.sync.dma_start(dst_list[:], offs2)
         nc.sync.dma_start(tab_w[:].bitcast(I32), tab_words[0].rearrange("p t i -> p (t i)").bitcast(I32))
-        nc.sync.dma_start(wc_w[:].bitcast(I32), wc_words[0].bitcast(I32))
-        load_scale_rows(wc_s, wc_scales)
         load_wb(0)
+        load_scale_rows(wc_s, wc_scales)
+        nc.sync.dma_start(wc_w[:].bitcast(I32), wc_words[0].bitcast(I32))
+        nc.sync.dma_start(wgo_rows[0:J_TILES, :], wgo[0, :].rearrange("(a b) -> a b", b=P))
         nc.sync.dma_start(wa_w[:].bitcast(I32), wa_words[0].bitcast(I32))
         load_scale_rows(wa_s, wa_scales)
-        with tc.tile_pool(name="mid", bufs=1) as mid:
-            wb_bf.append(mid.tile([P, 256 * PACK], BF16, name="wb_bf0", align_bytes=64))
-            round_wb(0)
-            wgo_cols = late.tile([P, J_TILES], F32, name="wgo_cols", tag="first")
+        load_wb(1)
 
-            wgo_acc = take_bank()
-            nc.tensor.transpose(wgo_acc[:, 0:P], wgo_rows[:], ident[:])
-            nc.scalar.copy(wgo_cols[:], wgo_acc[:, 0:J_TILES])
-            load_wb(1)
+        round_wb(0)
+        nc.tensor.transpose(bank_g[:, 0:P], wgo_rows[:], ident[:])
+        nc.scalar.copy(wgo_cols[:], bank_g[:, 0:J_TILES])
 
-            gather(src_s[:], tab_s, src_list, 0, J)
-            gather(dst_s[0][:], tab_s, dst_list, 0, HALF)
-            gather(src_w[:, 0:256], tab_w, src_list, 0, 256)
-            gather(src_w[:, 256:HALF], tab_w, src_list, 256, HALF)
-            gather(dst_w[0][:], tab_w, dst_list, 0, HALF)
-            gather(src_w[:, HALF:J], tab_w, src_list, HALF, J)
-            quantize_wb(0)
-        last = ctx.enter_context(tc.tile_pool(name="last", bufs=1))
-        for jt in range(4):
-            message_t(jt)
-        dst_s.append(last.tile([P, HALF], U8, name="dst_s1", align_bytes=64))
-        dst_w.append(last.tile([P, HALF], U32, name="dst_w1", align_bytes=64))
+        gather(src_s[0][:], tab_s, src_list, 0, HALF)
+        gather(dst_s[0][:], tab_s, dst_list, 0, HALF)
+        gather(src_w[0][:], tab_w, src_list, 0, HALF)
+        gather(dst_w[0][:], tab_w, dst_list, 0, HALF)
+        quantize_wb(0)
+        src_w.append(shared.tile([P, HALF], U32, name="src_w1", offset=16384, align_bytes=64))
+        src_s.append(shared.tile([P, HALF], U8, name="src_s1", offset=16384 + 2048, align_bytes=64))
+        dst_s.append(shared.tile([P, HALF], U8, name="dst_s1", offset=16384 + 2560, align_bytes=64))
+        dst_w.append(shared.tile([P, HALF], U32, name="dst_w1", offset=16384 + 3072, align_bytes=64))
+        gather(src_s[1][:], tab_s, src_list, HALF, J)
+        gather(src_w[1][:], tab_w, src_list, HALF, J)
         gather(dst_s[1][:], tab_s, dst_list, HALF, J)
         gather(dst_w[1][:], tab_w, dst_list, HALF, J)
-        page1 = late.tile([P, T], F32, name="page1", tag="wide", align_bytes=64)
-        pages.append(page1)
-        nc.gpsimd.memset(page1[:], 0.0)
-        message_back(0, 0)
-        gate(0, 0)
-        scatter(0, 0, HALF)
-        message_back(1, 0)
-        gate(1, 0)
-        scatter(1, 0, HALF)
-        for jt in range(4, 8):
-            message_t(jt)
+        for i in range(2):
+            pages.append(shared.tile([P, T], F32, name="page%d" % (i + 1), offset=8192 * i, align_bytes=64))
+            nc.gpsimd.memset(pages[i + 1][:], 0.0)
+
         for nt in range(2):
-            message_back(nt, 1)
-            gate(nt, 1)
+            half_tile(nt, 0)
+            scatter(nt, 0, HALF)
+        wb_bf.append(keep.tile([P, 256 * PACK], BF16, name="wb_bf1", tag="stage1", align_bytes=64))
+        round_wb(1)
+        quantize_wb(1)
+        for nt in range(2):
+            half_tile(nt, 1)
             scatter(nt, HALF, J)
             store(nt)
-            if nt == 0:
-                wb_bf.append(late.tile([P, 256 * PACK], BF16, name="wb_bf1", tag="wc", align_bytes=64))
-                round_wb(1)
-                quantize_wb(1)
-                page2 = late.tile([P, T], F32, name="page2", tag="wc", align_bytes=64)
-                pages.append(page2)
-                nc.gpsimd.memset(page2[:], 0.0)
         for nt in range(2, N_TILES):
             for h in range(2):
-                message_back(nt, h)
-                gate(nt, h)
+                half_tile(nt, h)
             scatter(nt, 0, J)
             store(nt)

@@ -43,7 +43,7 @@ def tile_list_rgg_none_kernel(
         dst_list = keep.tile([P, J // LIST_ROWS], U16, name="dst_list")
         tab_s = keep.tile([P, T], U8, name="tab_s", align_bytes=64)
         shared = ctx.enter_context(tc.tile_pool(name="shared", bufs=1))
-        tab_w = shared.tile([P, T], U32, name="tab_w", offset=4096, align_bytes=64)
+        tab_w = shared.tile([P, T], U32, name="tab_w", offset=0, align_bytes=64)
         wb_raw = [keep.tile([P, PACK, N // 2], F32, name="wb_raw%d" % i) for i in range(2)]
         wb_bf = [shared.tile([P, 256 * PACK], BF16, name="wb_bf0", offset=16384 + 1536, align_bytes=64)]
         wb_w = keep.tile([P, N], U32, name="wb_w", align_bytes=64)
@@ -97,7 +97,10 @@ def tile_list_rgg_none_kernel(
             nc.vector.quantize_mx(out=wb_w[:, cols].bitcast(FP8X4), scales=wb_s[:, cols], in_=wb_bf[i][:])
 
         def half_tile(nt, h):
-            stage = keep.tile([P, HALF], F32, name="stage", tag="stage%d" % (nt % 2), align_bytes=64)
+            if (nt, h) == (1, 0):
+                stage = shared.tile([P, HALF], F32, name="stage_early", offset=8192, align_bytes=64)
+            else:
+                stage = keep.tile([P, HALF], F32, name="stage", tag="stage%d" % h, align_bytes=64)
             cols = slice(h * HALF, (h + 1) * HALF)
             chans = slice(nt * P, (nt + 1) * P)
             for i in range(HALF // P):
@@ -185,16 +188,17 @@ def tile_list_rgg_none_kernel(
         gather(src_w[1][:], tab_w, src_list, HALF, J)
         gather(dst_s[1][:], tab_s, dst_list, HALF, J)
         gather(dst_w[1][:], tab_w, dst_list, HALF, J)
-        for i in range(2):
-            pages.append(shared.tile([P, T], F32, name="page%d" % (i + 1), offset=8192 * i, align_bytes=64))
-            nc.gpsimd.memset(pages[i + 1][:], 0.0)
+        pages.append(shared.tile([P, T], F32, name="page1", offset=0, align_bytes=64))
+        nc.gpsimd.memset(pages[1][:], 0.0)
 
         for nt in range(2):
             half_tile(nt, 0)
             scatter(nt, 0, HALF)
-        wb_bf.append(keep.tile([P, 256 * PACK], BF16, name="wb_bf1", tag="stage1", align_bytes=64))
+        wb_bf.append(shared.tile([P, 256 * PACK], BF16, name="wb_bf1", offset=8192, align_bytes=64))
         round_wb(1)
         quantize_wb(1)
+        pages.append(shared.tile([P, T], F32, name="page2", offset=8192, align_bytes=64))
+        nc.gpsimd.memset(pages[2][:], 0.0)
         for nt in range(2):
             half_tile(nt, 1)
             scatter(nt, HALF, J)

@@ -44,7 +44,7 @@ def tile_list_rgg_none_kernel(
         tab_s = keep.tile([P, T], U8, name="tab_s", align_bytes=64)
         shared = ctx.enter_context(tc.tile_pool(name="shared", bufs=1))
         tab_w = shared.tile([P, T], U32, name="tab_w", offset=0, align_bytes=64)
-        wb_raw = [keep.tile([P, PACK, N // 2], F32, name="wb_raw%d" % i) for i in range(2)]
+        wb_raw = [keep.tile([P, PACK, N // 2], F32, name="wb_raw", tag="stage%d" % (2 * i), align_bytes=64) for i in range(2)]
         wb_bf = [shared.tile([P, 256 * PACK], BF16, name="wb_bf0", offset=16384 + 1536, align_bytes=64)]
         wb_w = keep.tile([P, N], U32, name="wb_w", align_bytes=64)
         wb_s = keep.tile([P, N], U8, name="wb_s", align_bytes=64)
@@ -53,9 +53,9 @@ def tile_list_rgg_none_kernel(
         w_s = keep.tile([P, 2 * N], U8, name="w_s", align_bytes=64)
         wc_s = w_s[:, 0:N]
         wa_s = w_s[:, N : 2 * N]
-        src_s = [keep.tile([P, HALF], U8, name="src_s0", align_bytes=64)]
+        src_s = keep.tile([P, J], U8, name="src_s", align_bytes=64)
         dst_s = [keep.tile([P, HALF], U8, name="dst_s0", align_bytes=64)]
-        src_w = [keep.tile([P, HALF], U32, name="src_w0", align_bytes=64)]
+        src_w = [keep.tile([P, HALF], U32, name="src_w%d" % h, align_bytes=64) for h in range(2)]
         dst_w = [keep.tile([P, HALF], U32, name="dst_w0", align_bytes=64)]
         ident = keep.tile([P, P], F32, name="ident")
         wgo_rows = keep.tile([P, P], F32, name="wgo_rows")
@@ -107,7 +107,7 @@ def tile_list_rgg_none_kernel(
                 nc.tensor.matmul_mx(
                     out=bank_m[:, i * P : (i + 1) * P],
                     lhsT=src_w[h][:, i * P : (i + 1) * P].bitcast(FP8X4),
-                    lhsT_scale=src_s[h][:, i * P : (i + 1) * P],
+                    lhsT_scale=src_s[:, h * HALF + i * P : h * HALF + (i + 1) * P],
                     rhs=wc_w[:, 2 * nt * P : 2 * (nt + 1) * P].bitcast(FP4X4),
                     rhs_scale=wc_s[:, chans],
                     start=True,
@@ -118,28 +118,28 @@ def tile_list_rgg_none_kernel(
                 nc.scalar.activation(
                     stage[:, i * P : (i + 1) * P], bank_m[:, i * P : (i + 1) * P], COPY, scale=wgo_cols[:, jt : jt + 1]
                 )
-            nc.tensor.matmul_mx(
-                out=bank_g[:],
-                lhsT=wb_w[:, chans].bitcast(FP8X4),
-                lhsT_scale=wb_s[:, chans],
-                rhs=src_w[h][:].bitcast(FP8X4),
-                rhs_scale=src_s[h][:],
-                start=True,
-                stop=False,
-            )
+            for i in range(HALF // P):
+                nc.tensor.transpose(bank_t[:, i * P : (i + 1) * P], stage[:, i * P : (i + 1) * P], ident[:])
+            nc.scalar.copy(msw[nt][:, cols], bank_t[:])
             nc.tensor.matmul_mx(
                 out=bank_g[:],
                 lhsT=wa_w[:, 2 * nt * P : 2 * (nt + 1) * P].bitcast(FP4X4),
                 lhsT_scale=wa_s[:, chans],
                 rhs=dst_w[h][:].bitcast(FP8X4),
                 rhs_scale=dst_s[h][:],
+                start=True,
+                stop=False,
+            )
+            nc.tensor.matmul_mx(
+                out=bank_g[:],
+                lhsT=wb_w[:, chans].bitcast(FP8X4),
+                lhsT_scale=wb_s[:, chans],
+                rhs=src_w[h][:].bitcast(FP8X4),
+                rhs_scale=src_s[:, cols],
                 start=False,
                 stop=True,
             )
-            for i in range(HALF // P):
-                nc.tensor.transpose(bank_t[:, i * P : (i + 1) * P], stage[:, i * P : (i + 1) * P], ident[:])
             nc.scalar.activation(eta[nt][:, cols], bank_g[:], SIGMOID)
-            nc.scalar.copy(msw[nt][:, cols], bank_t[:])
 
         def scatter(nt, lo, hi):
             page = pages[nt % 3]
@@ -153,8 +153,8 @@ def tile_list_rgg_none_kernel(
                 nc.sync.dma_start(out[rows, 0 : T // 2], pages[nt % 3][:, 0 : T // 2])
                 nc.scalar.dma_start(out[rows, T // 2 : T], pages[nt % 3][:, T // 2 : T])
 
-        nc.vector.memset(w_s[:].bitcast(I32), 0)
         nc.vector.memset(wgo_rows[:], 0.0)
+        nc.vector.memset(w_s[:].bitcast(I32), 0)
         make_identity(nc, ident[:])
         nc.vector.memset(page0[:].bitcast(I32), 0)
         nc.scalar.activation(warm[:], page0[:, 0:1], SIGMOID)
@@ -162,30 +162,27 @@ def tile_list_rgg_none_kernel(
         nc.sync.dma_start(src_list[:], offs)
         load_table_scales()
         nc.sync.dma_start(dst_list[:], offs2)
+        nc.sync.dma_start(wgo_rows[0:J_TILES, :], wgo[0, :].rearrange("(a b) -> a b", b=P))
         nc.sync.dma_start(tab_w[:].bitcast(I32), tab_words[0].rearrange("p t i -> p (t i)").bitcast(I32))
-        load_wb(0)
         load_scale_rows(wc_s, wc_scales)
         nc.sync.dma_start(wc_w[:].bitcast(I32), wc_words[0].bitcast(I32))
-        nc.sync.dma_start(wgo_rows[0:J_TILES, :], wgo[0, :].rearrange("(a b) -> a b", b=P))
+        load_wb(0)
         nc.sync.dma_start(wa_w[:].bitcast(I32), wa_words[0].bitcast(I32))
         load_scale_rows(wa_s, wa_scales)
         load_wb(1)
 
-        round_wb(0)
         nc.tensor.transpose(bank_g[:, 0:P], wgo_rows[:], ident[:])
         nc.scalar.copy(wgo_cols[:], bank_g[:, 0:J_TILES])
+        round_wb(0)
 
-        gather(src_s[0][:], tab_s, src_list, 0, HALF)
+        gather(src_s[:], tab_s, src_list, 0, J)
         gather(dst_s[0][:], tab_s, dst_list, 0, HALF)
         gather(src_w[0][:], tab_w, src_list, 0, HALF)
         gather(dst_w[0][:], tab_w, dst_list, 0, HALF)
+        gather(src_w[1][:], tab_w, src_list, HALF, J)
         quantize_wb(0)
-        src_w.append(shared.tile([P, HALF], U32, name="src_w1", offset=16384, align_bytes=64))
-        src_s.append(shared.tile([P, HALF], U8, name="src_s1", offset=16384 + 2048, align_bytes=64))
         dst_s.append(shared.tile([P, HALF], U8, name="dst_s1", offset=16384 + 2560, align_bytes=64))
         dst_w.append(shared.tile([P, HALF], U32, name="dst_w1", offset=16384 + 3072, align_bytes=64))
-        gather(src_s[1][:], tab_s, src_list, HALF, J)
-        gather(src_w[1][:], tab_w, src_list, HALF, J)
         gather(dst_s[1][:], tab_s, dst_list, HALF, J)
         gather(dst_w[1][:], tab_w, dst_list, HALF, J)
         pages.append(shared.tile([P, T], F32, name="page1", offset=0, align_bytes=64))

@@ -1,7 +1,6 @@
 from contextlib import ExitStack
 
 import concourse.mybir as mybir
-from concourse.masks import make_identity
 
 K, N, T, J = 512, 512, 2048, 1024
 FLOPS = 3 * 2 * K * N * J
@@ -42,19 +41,8 @@ def tile_list_rgg_none_kernel(
         src_list = keep.tile([P, J // LIST_ROWS], U16, name="src_list")
         dst_list = keep.tile([P, J // LIST_ROWS], U16, name="dst_list")
         tab_s = keep.tile([P, T], U8, name="tab_s", align_bytes=64)
-        shared = ctx.enter_context(tc.tile_pool(name="shared", bufs=1))
-        tab_w = shared.tile([P, T], U32, name="tab_w", offset=0, align_bytes=64)
-        wb_raw = [keep.tile([P, PACK, N // 2], F32, name="wb_raw", tag="stage%d" % (2 * i), align_bytes=64) for i in range(2)]
-        wb_bf = [shared.tile([P, 256 * PACK], BF16, name="wb_bf0", offset=16384 + 1536, align_bytes=64)]
         wb_w = keep.tile([P, N], U32, name="wb_w", align_bytes=64)
         wb_s = keep.tile([P, N], U8, name="wb_s", align_bytes=64)
-        wc_w = keep.tile([P, 2 * N], U8, name="wc_w", align_bytes=64)
-        wa_w = keep.tile([P, 2 * N], U8, name="wa_w", align_bytes=64)
-        w_s = keep.tile([P, 2 * N], U8, name="w_s", align_bytes=64)
-        wc_s = w_s[:, 0:N]
-        wa_s = w_s[:, N : 2 * N]
-        src_s = keep.tile([P, J], U8, name="src_s", align_bytes=64)
-        dst_s = [keep.tile([P, HALF], U8, name="dst_s0", align_bytes=64)]
         src_w = [keep.tile([P, HALF], U32, name="src_w%d" % h, align_bytes=64) for h in range(2)]
         dst_w = [keep.tile([P, HALF], U32, name="dst_w0", align_bytes=64)]
         ident = keep.tile([P, P], F32, name="ident")
@@ -63,8 +51,30 @@ def tile_list_rgg_none_kernel(
         msw = [keep.tile([P, J], F32, name="msw%d" % nt) for nt in range(N_TILES)]
         eta = [keep.tile([P, J], F32, name="eta%d" % nt) for nt in range(N_TILES)]
         warm = keep.tile([P, 1], F32, name="warm")
-        page0 = keep.tile([P, T], F32, name="page0")
-        pages = [page0]
+
+        nc.vector.memset(tab_s[:].bitcast(I32), 0)
+        nc.vector.memset(wgo_rows[:], 0.0)
+        with tc.tile_pool(name="early", bufs=1) as early:
+            diag = early.tile([P, P], I32, name="diag")
+            nc.gpsimd.iota(diag[:], [[1, P]], base=0, channel_multiplier=-1)
+            nc.vector.tensor_scalar(ident[:], diag[:], 0.0, None, mybir.AluOpType.is_equal)
+
+        late = ctx.enter_context(tc.tile_pool(name="late", bufs=1))
+
+        def late_tile(shape, dtype, name, kib):
+            return late.tile(shape, dtype, name=name, offset=int(kib * 1024), align_bytes=64)
+
+        tab_w = late_tile([P, T], U32, "tab_w", 0)
+        wb_bf = [late_tile([P, 256 * PACK], BF16, "wb_bf0", 17.5)]
+        wb_raw = [late_tile([P, PACK, N // 2], F32, "wb_raw%d" % i, 22 + 4 * i) for i in range(2)]
+        wc_w = late_tile([P, 2 * N], U8, "wc_w", 30)
+        wa_w = late_tile([P, 2 * N], U8, "wa_w", 31)
+        w_s = late_tile([P, 2 * N], U8, "w_s", 32)
+        wc_s = w_s[:, 0:N]
+        wa_s = w_s[:, N : 2 * N]
+        src_s = late_tile([P, J], U8, "src_s", 33)
+        dst_s = [late_tile([P, HALF], U8, "dst_s0", 34)]
+        pages = [late_tile([P, T], F32, "page0", 35)]
 
         def load_scale_rows(plane, rows):
             for q in range(4):
@@ -72,9 +82,9 @@ def tile_list_rgg_none_kernel(
 
         def load_table_scales():
             for q in range(4):
-                rows = tab_scales[0, 4 * q : 4 * q + 4, :].bitcast(I32)
-                nc.sync.dma_start(
-                    tab_s[QUAD * q : QUAD * (q + 1)].bitcast(I32), rows.unsqueeze(0).to_broadcast([QUAD // 4, 4, T // 4])
+                queue = nc.sync if q < 2 else nc.scalar
+                queue.dma_start(
+                    tab_s[QUAD * q : QUAD * q + 4].bitcast(I32), tab_scales[0, 4 * q : 4 * q + 4, :].bitcast(I32)
                 )
 
         def load_wb(i):
@@ -97,8 +107,10 @@ def tile_list_rgg_none_kernel(
             nc.vector.quantize_mx(out=wb_w[:, cols].bitcast(FP8X4), scales=wb_s[:, cols], in_=wb_bf[i][:])
 
         def half_tile(nt, h):
-            if (nt, h) == (1, 0):
-                stage = shared.tile([P, HALF], F32, name="stage_early", offset=8192, align_bytes=64)
+            if (nt, h) == (0, 0):
+                stage = late_tile([P, HALF], F32, "stage_first", 22)
+            elif (nt, h) == (1, 0):
+                stage = late_tile([P, HALF], F32, "stage_second", 8)
             else:
                 stage = keep.tile([P, HALF], F32, name="stage", tag="stage%d" % h, align_bytes=64)
             cols = slice(h * HALF, (h + 1) * HALF)
@@ -153,15 +165,13 @@ def tile_list_rgg_none_kernel(
                 nc.sync.dma_start(out[rows, 0 : T // 2], pages[nt % 3][:, 0 : T // 2])
                 nc.scalar.dma_start(out[rows, T // 2 : T], pages[nt % 3][:, T // 2 : T])
 
-        nc.vector.memset(wgo_rows[:], 0.0)
         nc.vector.memset(w_s[:].bitcast(I32), 0)
-        make_identity(nc, ident[:])
-        nc.vector.memset(page0[:].bitcast(I32), 0)
-        nc.scalar.activation(warm[:], page0[:, 0:1], SIGMOID)
+        nc.vector.memset(pages[0][:].bitcast(I32), 0)
 
         nc.sync.dma_start(src_list[:], offs)
         load_table_scales()
         nc.sync.dma_start(dst_list[:], offs2)
+        nc.scalar.activation(warm[:], ident[:, 0:1], SIGMOID)
         nc.sync.dma_start(wgo_rows[0:J_TILES, :], wgo[0, :].rearrange("(a b) -> a b", b=P))
         nc.sync.dma_start(tab_w[:].bitcast(I32), tab_words[0].rearrange("p t i -> p (t i)").bitcast(I32))
         load_scale_rows(wc_s, wc_scales)
@@ -181,20 +191,20 @@ def tile_list_rgg_none_kernel(
         gather(dst_w[0][:], tab_w, dst_list, 0, HALF)
         gather(src_w[1][:], tab_w, src_list, HALF, J)
         quantize_wb(0)
-        dst_s.append(shared.tile([P, HALF], U8, name="dst_s1", offset=16384 + 2560, align_bytes=64))
-        dst_w.append(shared.tile([P, HALF], U32, name="dst_w1", offset=16384 + 3072, align_bytes=64))
+        dst_s.append(late_tile([P, HALF], U8, "dst_s1", 18.5))
+        dst_w.append(late_tile([P, HALF], U32, "dst_w1", 19))
         gather(dst_s[1][:], tab_s, dst_list, HALF, J)
         gather(dst_w[1][:], tab_w, dst_list, HALF, J)
-        pages.append(shared.tile([P, T], F32, name="page1", offset=0, align_bytes=64))
+        pages.append(late_tile([P, T], F32, "page1", 0))
         nc.gpsimd.memset(pages[1][:], 0.0)
 
         for nt in range(2):
             half_tile(nt, 0)
             scatter(nt, 0, HALF)
-        wb_bf.append(shared.tile([P, 256 * PACK], BF16, name="wb_bf1", offset=8192, align_bytes=64))
+        wb_bf.append(late_tile([P, 256 * PACK], BF16, "wb_bf1", 8))
         round_wb(1)
         quantize_wb(1)
-        pages.append(shared.tile([P, T], F32, name="page2", offset=8192, align_bytes=64))
+        pages.append(late_tile([P, T], F32, "page2", 8))
         nc.gpsimd.memset(pages[2][:], 0.0)
         for nt in range(2):
             half_tile(nt, 1)

@@ -115,9 +115,10 @@ def tile_list_rgg_none_kernel(
                 stage = keep.tile([P, HALF], F32, name="stage", tag="stage%d" % h, align_bytes=64)
             cols = slice(h * HALF, (h + 1) * HALF)
             chans = slice(nt * P, (nt + 1) * P)
+            acc = [bank_g if (nt, h) == (0, 0) and i < 2 else bank_m for i in range(HALF // P)]
             for i in range(HALF // P):
                 nc.tensor.matmul_mx(
-                    out=bank_m[:, i * P : (i + 1) * P],
+                    out=acc[i][:, i * P : (i + 1) * P],
                     lhsT=src_w[h][:, i * P : (i + 1) * P].bitcast(FP8X4),
                     lhsT_scale=src_s[:, h * HALF + i * P : h * HALF + (i + 1) * P],
                     rhs=wc_w[:, 2 * nt * P : 2 * (nt + 1) * P].bitcast(FP4X4),
@@ -128,7 +129,7 @@ def tile_list_rgg_none_kernel(
             for i in range(HALF // P):
                 jt = h * (HALF // P) + i
                 nc.scalar.activation(
-                    stage[:, i * P : (i + 1) * P], bank_m[:, i * P : (i + 1) * P], COPY, scale=wgo_cols[:, jt : jt + 1]
+                    stage[:, i * P : (i + 1) * P], acc[i][:, i * P : (i + 1) * P], COPY, scale=wgo_cols[:, jt : jt + 1]
                 )
             for i in range(HALF // P):
                 nc.tensor.transpose(bank_t[:, i * P : (i + 1) * P], stage[:, i * P : (i + 1) * P], ident[:])
@@ -181,8 +182,8 @@ def tile_list_rgg_none_kernel(
         load_scale_rows(wa_s, wa_scales)
         load_wb(1)
 
-        nc.tensor.transpose(bank_g[:, 0:P], wgo_rows[:], ident[:])
-        nc.scalar.copy(wgo_cols[:], bank_g[:, 0:J_TILES])
+        nc.tensor.transpose(bank_t[:, 0:P], wgo_rows[:], ident[:])
+        nc.scalar.copy(wgo_cols[:], bank_t[:, 0:J_TILES])
         round_wb(0)
 
         gather(src_s[:], tab_s, src_list, 0, J)

@@ -66,15 +66,15 @@ def tile_list_rgg_none_kernel(
 
         tab_w = late_tile([P, T], U32, "tab_w", 0)
         wb_bf = [late_tile([P, 256 * PACK], BF16, "wb_bf0", 17.5)]
-        wb_raw = [late_tile([P, PACK, N // 2], F32, "wb_raw%d" % i, 22 + 4 * i) for i in range(2)]
-        wc_w = late_tile([P, 2 * N], U8, "wc_w", 30)
-        wa_w = late_tile([P, 2 * N], U8, "wa_w", 31)
-        w_s = late_tile([P, 2 * N], U8, "w_s", 32)
+        wb_raw = [late_tile([P, PACK, N // 2], F32, "wb_raw%d" % i, 22 + 6 * i) for i in range(2)]
+        wc_w = late_tile([P, 2 * N], U8, "wc_w", 32)
+        wa_w = late_tile([P, 2 * N], U8, "wa_w", 33)
+        w_s = late_tile([P, 2 * N], U8, "w_s", 34)
         wc_s = w_s[:, 0:N]
         wa_s = w_s[:, N : 2 * N]
-        src_s = late_tile([P, J], U8, "src_s", 33)
-        dst_s = [late_tile([P, HALF], U8, "dst_s0", 34)]
-        pages = [late_tile([P, T], F32, "page0", 35)]
+        src_s = late_tile([P, J], U8, "src_s", 35)
+        dst_s = [late_tile([P, HALF], U8, "dst_s0", 36)]
+        pages = [late_tile([P, T], F32, "page0", 37)]
 
         def load_scale_rows(plane, rows):
             for q in range(4):
@@ -160,11 +160,7 @@ def tile_list_rgg_none_kernel(
 
         def store(nt):
             rows = slice(nt * P, (nt + 1) * P)
-            if nt < N_TILES - 1:
-                nc.sync.dma_start(out[rows, :], pages[nt % 3][:])
-            else:
-                nc.sync.dma_start(out[rows, 0 : T // 2], pages[nt % 3][:, 0 : T // 2])
-                nc.scalar.dma_start(out[rows, T // 2 : T], pages[nt % 3][:, T // 2 : T])
+            nc.sync.dma_start(out[rows, :], pages[nt % 3][:])
 
         nc.vector.memset(w_s[:].bitcast(I32), 0)
         nc.vector.memset(pages[0][:].bitcast(I32), 0)
@@ -192,8 +188,8 @@ def tile_list_rgg_none_kernel(
         gather(dst_w[0][:], tab_w, dst_list, 0, HALF)
         gather(src_w[1][:], tab_w, src_list, HALF, J)
         quantize_wb(0)
-        dst_s.append(late_tile([P, HALF], U8, "dst_s1", 18.5))
-        dst_w.append(late_tile([P, HALF], U32, "dst_w1", 19))
+        dst_s.append(late_tile([P, HALF], U8, "dst_s1", 25))
+        dst_w.append(late_tile([P, HALF], U32, "dst_w1", 25.5))
         gather(dst_s[1][:], tab_s, dst_list, HALF, J)
         gather(dst_w[1][:], tab_w, dst_list, HALF, J)
         pages.append(late_tile([P, T], F32, "page1", 0))

@@ -34,9 +34,9 @@ def tile_list_rgg_none_kernel(
     with ExitStack() as ctx:
         keep = ctx.enter_context(tc.tile_pool(name="keep", bufs=1))
         psum = ctx.enter_context(tc.psum_pool(name="psum", bufs=1))
-        bank_m = psum.tile([P, HALF], F32, name="bank_m")
-        bank_g = psum.tile([P, HALF], F32, name="bank_g")
-        bank_t = psum.tile([P, HALF], F32, name="bank_t")
+        banks_m = [psum.tile([P, HALF], F32, name="bank_m%d" % i) for i in range(2)]
+        banks_g = [psum.tile([P, HALF], F32, name="bank_g%d" % i) for i in range(2)]
+        banks_t = [psum.tile([P, HALF], F32, name="bank_t%d" % i) for i in range(2)]
 
         src_list = keep.tile([P, J // LIST_ROWS], U16, name="src_list")
         dst_list = keep.tile([P, J // LIST_ROWS], U16, name="dst_list")
@@ -107,12 +107,16 @@ def tile_list_rgg_none_kernel(
             nc.vector.quantize_mx(out=wb_w[:, cols].bitcast(FP8X4), scales=wb_s[:, cols], in_=wb_bf[i][:])
 
         def half_tile(nt, h):
+            unit = 2 * h + nt if nt < 2 else 2 * nt + h
+            bank_m = banks_m[0] if unit < 2 else banks_m[(unit + 1) % 2]
+            bank_g = banks_g[0] if unit < 2 else banks_g[(unit + 1) % 2]
+            bank_t = [banks_m[1], banks_g[1]][unit] if unit < 2 else banks_t[unit % 2]
             if (nt, h) == (0, 0):
                 stage = late_tile([P, HALF], F32, "stage_first", 22)
             elif (nt, h) == (1, 0):
                 stage = late_tile([P, HALF], F32, "stage_second", 8)
             else:
-                stage = keep.tile([P, HALF], F32, name="stage", tag="stage%d" % h, align_bytes=64)
+                stage = keep.tile([P, HALF], F32, name="stage", tag="stage%d" % (unit % 2), align_bytes=64)
             cols = slice(h * HALF, (h + 1) * HALF)
             chans = slice(nt * P, (nt + 1) * P)
             acc = [bank_g if (nt, h) == (0, 0) and i < 2 else bank_m for i in range(HALF // P)]
@@ -178,8 +182,8 @@ def tile_list_rgg_none_kernel(
         load_scale_rows(wa_s, wa_scales)
         load_wb(1)
 
-        nc.tensor.transpose(bank_t[:, 0:P], wgo_rows[:], ident[:])
-        nc.scalar.copy(wgo_cols[:], bank_t[:, 0:J_TILES])
+        nc.tensor.transpose(banks_m[1][:, 0:P], wgo_rows[:], ident[:])
+        nc.scalar.copy(wgo_cols[:], banks_m[1][:, 0:J_TILES])
         round_wb(0)
 
         gather(src_s[:], tab_s, src_list, 0, J)

@@ -1,6 +1,7 @@
 from contextlib import ExitStack
 
 import concourse.mybir as mybir
+from concourse.masks import make_identity
 
 K, N, T, J = 512, 512, 2048, 1024
 FLOPS = 3 * 2 * K * N * J
@@ -24,6 +25,8 @@ N_TILES = N // P
 J_TILES = J // P
 LIST_ROWS = 16
 QUAD = 32
+SCALE_ROWS = 16
+FIRST_ROW = P - SCALE_ROWS
 
 
 def tile_list_rgg_none_kernel(
@@ -33,6 +36,7 @@ def tile_list_rgg_none_kernel(
 
     with ExitStack() as ctx:
         keep = ctx.enter_context(tc.tile_pool(name="keep", bufs=1))
+        work = ctx.enter_context(tc.tile_pool(name="work", bufs=1))
         psum = ctx.enter_context(tc.psum_pool(name="psum", bufs=1))
         banks_m = [psum.tile([P, HALF], F32, name="bank_m%d" % i) for i in range(2)]
         banks_g = [psum.tile([P, HALF], F32, name="bank_g%d" % i) for i in range(2)]
@@ -41,51 +45,43 @@ def tile_list_rgg_none_kernel(
         src_list = keep.tile([P, J // LIST_ROWS], U16, name="src_list")
         dst_list = keep.tile([P, J // LIST_ROWS], U16, name="dst_list")
         tab_s = keep.tile([P, T], U8, name="tab_s", align_bytes=64)
+        planes = keep.tile([P, 2 * J], U8, name="planes", align_bytes=64)
+        w_s = keep.tile([P, 2 * N], U8, name="w_s", align_bytes=64)
+        wc_w = keep.tile([P, 2 * N], U8, name="wc_w", align_bytes=64)
+        wa_w = keep.tile([P, 2 * N], U8, name="wa_w", align_bytes=64)
         wb_w = keep.tile([P, N], U32, name="wb_w", align_bytes=64)
         wb_s = keep.tile([P, N], U8, name="wb_s", align_bytes=64)
         src_w = [keep.tile([P, HALF], U32, name="src_w%d" % h, align_bytes=64) for h in range(2)]
         dst_w = [keep.tile([P, HALF], U32, name="dst_w0", align_bytes=64)]
         ident = keep.tile([P, P], F32, name="ident")
-        wgo_rows = keep.tile([P, P], F32, name="wgo_rows")
         wgo_cols = keep.tile([P, J_TILES], F32, name="wgo_cols")
         msw = [keep.tile([P, J], F32, name="msw%d" % nt) for nt in range(N_TILES)]
         eta = [keep.tile([P, J], F32, name="eta%d" % nt) for nt in range(N_TILES)]
+        warm_in = keep.tile([P, 1], F32, name="warm_in")
         warm = keep.tile([P, 1], F32, name="warm")
-
-        nc.vector.memset(tab_s[:].bitcast(I32), 0)
-        nc.vector.memset(wgo_rows[:], 0.0)
-        with tc.tile_pool(name="early", bufs=1) as early:
-            diag = early.tile([P, P], I32, name="diag")
-            nc.gpsimd.iota(diag[:], [[1, P]], base=0, channel_multiplier=-1)
-            nc.vector.tensor_scalar(ident[:], diag[:], 0.0, None, mybir.AluOpType.is_equal)
-
-        late = ctx.enter_context(tc.tile_pool(name="late", bufs=1))
-
-        def late_tile(shape, dtype, name, kib):
-            return late.tile(shape, dtype, name=name, offset=int(kib * 1024), align_bytes=64)
-
-        tab_w = late_tile([P, T], U32, "tab_w", 0)
-        wb_bf = [late_tile([P, 256 * PACK], BF16, "wb_bf0", 17.5)]
-        wb_raw = [late_tile([P, PACK, N // 2], F32, "wb_raw%d" % i, 22 + 6 * i) for i in range(2)]
-        wc_w = late_tile([P, 2 * N], U8, "wc_w", 32)
-        wa_w = late_tile([P, 2 * N], U8, "wa_w", 33)
-        w_s = late_tile([P, 2 * N], U8, "w_s", 34)
         wc_s = w_s[:, 0:N]
         wa_s = w_s[:, N : 2 * N]
-        src_s = late_tile([P, J], U8, "src_s", 35)
-        dst_s = [late_tile([P, HALF], U8, "dst_s0", 36)]
-        pages = [late_tile([P, T], F32, "page0", 37)]
+        src_s = planes[:, 0:J]
+        dst_s = planes[:, J : 2 * J]
 
-        def load_scale_rows(plane, rows):
-            for q in range(4):
-                nc.sync.dma_start(plane[QUAD * q : QUAD * q + 4].bitcast(I32), rows[0, 4 * q : 4 * q + 4, :].bitcast(I32))
+        def placed(shape, dtype, name, kib):
+            return work.tile(shape, dtype, name=name, offset=int(kib * 1024), align_bytes=64)
 
-        def load_table_scales():
+        tab_w = placed([P, T], U32, "tab_w", 0)
+        wb_bf = [placed([P, 256 * PACK], BF16, "wb_bf0", 16)]
+        wb_raw = [placed([P, PACK, N // 2], F32, "wb_raw0", 18)]
+        picked_src = placed([P, J], U8, "picked_src", 23)
+        picked_dst = placed([P, HALF], U8, "picked_dst", 24)
+        wgo_rows = placed([P, P], F32, "wgo_rows", 32)
+
+        def load_scale_rows(queue, plane, rows):
             for q in range(4):
-                queue = nc.sync if q < 2 else nc.scalar
-                queue.dma_start(
-                    tab_s[QUAD * q : QUAD * q + 4].bitcast(I32), tab_scales[0, 4 * q : 4 * q + 4, :].bitcast(I32)
-                )
+                queue.dma_start(plane[QUAD * q : QUAD * q + 4].bitcast(I32), rows[0, 4 * q : 4 * q + 4, :].bitcast(I32))
+
+        def move_scale_rows(plane, rows):
+            for q in range(4):
+                lo = FIRST_ROW + 4 * q
+                nc.sync.dma_start(plane[QUAD * q : QUAD * q + 4].bitcast(I32), rows[lo : lo + 4].bitcast(I32))
 
         def load_wb(i):
             nc.sync.dma_start(wb_raw[i][:], wb.rearrange("(p t) n -> p t n", t=PACK)[:, :, i * 256 : (i + 1) * 256])
@@ -111,15 +107,15 @@ def tile_list_rgg_none_kernel(
             bank_m = banks_m[0] if unit < 2 else banks_m[(unit + 1) % 2]
             bank_g = banks_g[0] if unit < 2 else banks_g[(unit + 1) % 2]
             bank_t = [banks_m[1], banks_g[1]][unit] if unit < 2 else banks_t[unit % 2]
-            if (nt, h) == (0, 0):
-                stage = late_tile([P, HALF], F32, "stage_first", 22)
-            elif (nt, h) == (1, 0):
-                stage = late_tile([P, HALF], F32, "stage_second", 8)
+            if unit == 0:
+                stage = placed([P, HALF], F32, "stage_first", 18)
+            elif unit == 1:
+                stage = placed([P, HALF], F32, "stage_second", 8)
             else:
                 stage = keep.tile([P, HALF], F32, name="stage", tag="stage%d" % (unit % 2), align_bytes=64)
             cols = slice(h * HALF, (h + 1) * HALF)
             chans = slice(nt * P, (nt + 1) * P)
-            acc = [bank_g if (nt, h) == (0, 0) and i < 2 else bank_m for i in range(HALF // P)]
+            acc = [bank_g if unit == 0 and i < 2 else bank_m for i in range(HALF // P)]
             for i in range(HALF // P):
                 nc.tensor.matmul_mx(
                     out=acc[i][:, i * P : (i + 1) * P],
@@ -143,7 +139,7 @@ def tile_list_rgg_none_kernel(
                 lhsT=wa_w[:, 2 * nt * P : 2 * (nt + 1) * P].bitcast(FP4X4),
                 lhsT_scale=wa_s[:, chans],
                 rhs=dst_w[h][:].bitcast(FP8X4),
-                rhs_scale=dst_s[h][:],
+                rhs_scale=dst_s[:, cols],
                 start=True,
                 stop=False,
             )
@@ -167,45 +163,56 @@ def tile_list_rgg_none_kernel(
             nc.sync.dma_start(out[rows, :], pages[nt % 3][:])
 
         nc.vector.memset(w_s[:].bitcast(I32), 0)
-        nc.vector.memset(pages[0][:].bitcast(I32), 0)
+        nc.vector.memset(warm_in[:], 0.0)
+        nc.vector.memset(tab_s[0:FIRST_ROW].bitcast(I32), 0)
+        nc.vector.memset(wgo_rows[:], 0.0)
+        nc.vector.memset(planes[:].bitcast(I32), 0)
+        nc.vector.memset(ident[:], 0.0)
+        make_identity(nc, ident[:], nomemset=True)
 
+        nc.sync.dma_start(tab_s[FIRST_ROW:P].bitcast(I32), tab_scales[0].bitcast(I32))
         nc.sync.dma_start(src_list[:], offs)
-        load_table_scales()
         nc.sync.dma_start(dst_list[:], offs2)
-        nc.scalar.activation(warm[:], ident[:, 0:1], SIGMOID)
-        nc.sync.dma_start(wgo_rows[0:J_TILES, :], wgo[0, :].rearrange("(a b) -> a b", b=P))
+        nc.scalar.activation(warm[:], warm_in[:], SIGMOID)
         nc.sync.dma_start(tab_w[:].bitcast(I32), tab_words[0].rearrange("p t i -> p (t i)").bitcast(I32))
-        load_scale_rows(wc_s, wc_scales)
+        load_scale_rows(nc.sync, wc_s, wc_scales)
         nc.sync.dma_start(wc_w[:].bitcast(I32), wc_words[0].bitcast(I32))
+        nc.sync.dma_start(wgo_rows[0:J_TILES, :], wgo[0, :].rearrange("(a b) -> a b", b=P))
         load_wb(0)
         nc.sync.dma_start(wa_w[:].bitcast(I32), wa_words[0].bitcast(I32))
-        load_scale_rows(wa_s, wa_scales)
-        load_wb(1)
+        load_scale_rows(nc.gpsimd, wa_s, wa_scales)
 
         nc.tensor.transpose(banks_m[1][:, 0:P], wgo_rows[:], ident[:])
         nc.scalar.copy(wgo_cols[:], banks_m[1][:, 0:J_TILES])
+        pages = [placed([P, T], F32, "page0", 32)]
+        nc.gpsimd.memset(pages[0][:], 0.0)
         round_wb(0)
 
-        gather(src_s[:], tab_s, src_list, 0, J)
-        gather(dst_s[0][:], tab_s, dst_list, 0, HALF)
+        gather(picked_src[:], tab_s, src_list, 0, J)
+        move_scale_rows(src_s, picked_src)
+        gather(picked_dst[:], tab_s, dst_list, 0, HALF)
+        move_scale_rows(dst_s[:, 0:HALF], picked_dst)
+        wb_raw.append(placed([P, PACK, N // 2], F32, "wb_raw1", 23))
+        load_wb(1)
         gather(src_w[0][:], tab_w, src_list, 0, HALF)
         gather(dst_w[0][:], tab_w, dst_list, 0, HALF)
         gather(src_w[1][:], tab_w, src_list, HALF, J)
         quantize_wb(0)
-        dst_s.append(late_tile([P, HALF], U8, "dst_s1", 25))
-        dst_w.append(late_tile([P, HALF], U32, "dst_w1", 25.5))
-        gather(dst_s[1][:], tab_s, dst_list, HALF, J)
+        picked_late = placed([P, HALF], U8, "picked_late", 20)
+        dst_w.append(placed([P, HALF], U32, "dst_w1", 20.5))
+        gather(picked_late[:], tab_s, dst_list, HALF, J)
+        move_scale_rows(dst_s[:, HALF:J], picked_late)
         gather(dst_w[1][:], tab_w, dst_list, HALF, J)
-        pages.append(late_tile([P, T], F32, "page1", 0))
+        pages.append(placed([P, T], F32, "page1", 0))
         nc.gpsimd.memset(pages[1][:], 0.0)
 
         for nt in range(2):
             half_tile(nt, 0)
             scatter(nt, 0, HALF)
-        wb_bf.append(late_tile([P, 256 * PACK], BF16, "wb_bf1", 8))
+        wb_bf.append(placed([P, 256 * PACK], BF16, "wb_bf1", 8))
         round_wb(1)
         quantize_wb(1)
-        pages.append(late_tile([P, T], F32, "page2", 8))
+        pages.append(placed([P, T], F32, "page2", 8))
         nc.gpsimd.memset(pages[2][:], 0.0)
         for nt in range(2):
             half_tile(nt, 1)

@@ -1,7 +1,6 @@
 from contextlib import ExitStack
 
 import concourse.mybir as mybir
-from concourse.masks import make_identity
 
 K, N, T, J = 512, 512, 2048, 1024
 FLOPS = 3 * 2 * K * N * J
@@ -36,43 +35,55 @@ def tile_list_rgg_none_kernel(
 
     with ExitStack() as ctx:
         keep = ctx.enter_context(tc.tile_pool(name="keep", bufs=1))
-        work = ctx.enter_context(tc.tile_pool(name="work", bufs=1))
         psum = ctx.enter_context(tc.psum_pool(name="psum", bufs=1))
-        banks_m = [psum.tile([P, HALF], F32, name="bank_m%d" % i) for i in range(2)]
-        banks_g = [psum.tile([P, HALF], F32, name="bank_g%d" % i) for i in range(2)]
-        banks_t = [psum.tile([P, HALF], F32, name="bank_t%d" % i) for i in range(2)]
+        words = ctx.enter_context(tc.tile_pool(name="words", bufs=1))
+        bank_m = psum.tile([P, HALF], F32, name="bank_m")
+        turns = [psum.tile([P, HALF], F32, name="turn%d" % i) for i in range(2)]
 
         src_list = keep.tile([P, J // LIST_ROWS], U16, name="src_list")
         dst_list = keep.tile([P, J // LIST_ROWS], U16, name="dst_list")
         tab_s = keep.tile([P, T], U8, name="tab_s", align_bytes=64)
         planes = keep.tile([P, 2 * J], U8, name="planes", align_bytes=64)
         w_s = keep.tile([P, 2 * N], U8, name="w_s", align_bytes=64)
-        wc_w = keep.tile([P, 2 * N], U8, name="wc_w", align_bytes=64)
-        wa_w = keep.tile([P, 2 * N], U8, name="wa_w", align_bytes=64)
+        wc_s = w_s[:, 0:N]
+        wa_s = w_s[:, N : 2 * N]
         wb_w = keep.tile([P, N], U32, name="wb_w", align_bytes=64)
         wb_s = keep.tile([P, N], U8, name="wb_s", align_bytes=64)
-        src_w = [keep.tile([P, HALF], U32, name="src_w%d" % h, align_bytes=64) for h in range(2)]
-        dst_w = [keep.tile([P, HALF], U32, name="dst_w0", align_bytes=64)]
         ident = keep.tile([P, P], F32, name="ident")
+        wgo_rows = keep.tile([P, P], F32, name="wgo_rows")
         wgo_cols = keep.tile([P, J_TILES], F32, name="wgo_cols")
         msw = [keep.tile([P, J], F32, name="msw%d" % nt) for nt in range(N_TILES)]
         eta = [keep.tile([P, J], F32, name="eta%d" % nt) for nt in range(N_TILES)]
         warm_in = keep.tile([P, 1], F32, name="warm_in")
         warm = keep.tile([P, 1], F32, name="warm")
-        wc_s = w_s[:, 0:N]
-        wa_s = w_s[:, N : 2 * N]
         src_s = planes[:, 0:J]
         dst_s = planes[:, J : 2 * J]
 
-        def placed(shape, dtype, name, kib):
-            return work.tile(shape, dtype, name=name, offset=int(kib * 1024), align_bytes=64)
+        tab_w = words.tile([P, T], U32, name="tab_w", offset=0, align_bytes=64)
 
-        tab_w = placed([P, T], U32, "tab_w", 0)
+        nc.vector.memset(w_s[:].bitcast(I32), 0)
+        nc.vector.memset(warm_in[:], 0.0)
+        nc.vector.memset(tab_s[0:FIRST_ROW].bitcast(I32), 0)
+        nc.vector.memset(wgo_rows[:], 0.0)
+        nc.vector.memset(planes[:].bitcast(I32), 0)
+        with tc.tile_pool(name="early", bufs=1) as early:
+            diag = early.tile([P, P], I32, name="diag")
+            nc.gpsimd.iota(diag[:], [[1, P]], base=0, channel_multiplier=-1)
+            nc.vector.tensor_scalar(ident[:], diag[:], 0.0, None, mybir.AluOpType.is_equal)
+
+        late = ctx.enter_context(tc.tile_pool(name="late", bufs=1))
+
+        def placed(shape, dtype, name, kib):
+            return late.tile(shape, dtype, name=name, offset=int(kib * 1024), align_bytes=64)
+
         wb_bf = [placed([P, 256 * PACK], BF16, "wb_bf0", 16)]
         wb_raw = [placed([P, PACK, N // 2], F32, "wb_raw0", 18)]
+        wc_w = placed([P, 2 * N], U8, "wc_w", 0)
+        wa_w = placed([P, 2 * N], U8, "wa_w", 1)
+        src_w = [placed([P, HALF], U32, "src_w%d" % h, 2 + 2 * h) for h in range(2)]
+        dst_w = [placed([P, HALF], U32, "dst_w0", 6)]
         picked_src = placed([P, J], U8, "picked_src", 23)
         picked_dst = placed([P, HALF], U8, "picked_dst", 24)
-        wgo_rows = placed([P, P], F32, "wgo_rows", 32)
 
         def load_scale_rows(queue, plane, rows):
             for q in range(4):
@@ -102,11 +113,8 @@ def tile_list_rgg_none_kernel(
             cols = slice(i * 256, (i + 1) * 256)
             nc.vector.quantize_mx(out=wb_w[:, cols].bitcast(FP8X4), scales=wb_s[:, cols], in_=wb_bf[i][:])
 
-        def half_tile(nt, h):
-            unit = 2 * h + nt if nt < 2 else 2 * nt + h
-            bank_m = banks_m[0] if unit < 2 else banks_m[(unit + 1) % 2]
-            bank_g = banks_g[0] if unit < 2 else banks_g[(unit + 1) % 2]
-            bank_t = [banks_m[1], banks_g[1]][unit] if unit < 2 else banks_t[unit % 2]
+        def make_unit(unit, nt, h):
+            bank_t, bank_g = turns[unit % 2], turns[(unit + 1) % 2]
             if unit == 0:
                 stage = placed([P, HALF], F32, "stage_first", 18)
             elif unit == 1:
@@ -162,30 +170,23 @@ def tile_list_rgg_none_kernel(
             rows = slice(nt * P, (nt + 1) * P)
             nc.sync.dma_start(out[rows, :], pages[nt % 3][:])
 
-        nc.vector.memset(w_s[:].bitcast(I32), 0)
-        nc.vector.memset(warm_in[:], 0.0)
-        nc.vector.memset(tab_s[0:FIRST_ROW].bitcast(I32), 0)
-        nc.vector.memset(wgo_rows[:], 0.0)
-        nc.vector.memset(planes[:].bitcast(I32), 0)
-        nc.vector.memset(ident[:], 0.0)
-        make_identity(nc, ident[:], nomemset=True)
-
         nc.sync.dma_start(tab_s[FIRST_ROW:P].bitcast(I32), tab_scales[0].bitcast(I32))
         nc.sync.dma_start(src_list[:], offs)
         nc.sync.dma_start(dst_list[:], offs2)
         nc.scalar.activation(warm[:], warm_in[:], SIGMOID)
         nc.sync.dma_start(tab_w[:].bitcast(I32), tab_words[0].rearrange("p t i -> p (t i)").bitcast(I32))
         load_scale_rows(nc.sync, wc_s, wc_scales)
-        nc.sync.dma_start(wc_w[:].bitcast(I32), wc_words[0].bitcast(I32))
         nc.sync.dma_start(wgo_rows[0:J_TILES, :], wgo[0, :].rearrange("(a b) -> a b", b=P))
         load_wb(0)
+        nc.sync.dma_start(wc_w[:].bitcast(I32), wc_words[0].bitcast(I32))
         nc.sync.dma_start(wa_w[:].bitcast(I32), wa_words[0].bitcast(I32))
-        load_scale_rows(nc.gpsimd, wa_s, wa_scales)
 
-        nc.tensor.transpose(banks_m[1][:, 0:P], wgo_rows[:], ident[:])
-        nc.scalar.copy(wgo_cols[:], banks_m[1][:, 0:J_TILES])
+        load_scale_rows(nc.gpsimd, wa_s, wa_scales)
         pages = [placed([P, T], F32, "page0", 32)]
         nc.gpsimd.memset(pages[0][:], 0.0)
+
+        nc.tensor.transpose(turns[0][:, 0:P], wgo_rows[:], ident[:])
+        nc.scalar.copy(wgo_cols[:], turns[0][:, 0:J_TILES])
         round_wb(0)
 
         gather(picked_src[:], tab_s, src_list, 0, J)
@@ -203,11 +204,11 @@ def tile_list_rgg_none_kernel(
         gather(picked_late[:], tab_s, dst_list, HALF, J)
         move_scale_rows(dst_s[:, HALF:J], picked_late)
         gather(dst_w[1][:], tab_w, dst_list, HALF, J)
-        pages.append(placed([P, T], F32, "page1", 0))
+        pages.append(words.tile([P, T], F32, name="page1", offset=0, align_bytes=64))
         nc.gpsimd.memset(pages[1][:], 0.0)
 
         for nt in range(2):
-            half_tile(nt, 0)
+            make_unit(nt, nt, 0)
             scatter(nt, 0, HALF)
         wb_bf.append(placed([P, 256 * PACK], BF16, "wb_bf1", 8))
         round_wb(1)
@@ -215,11 +216,11 @@ def tile_list_rgg_none_kernel(
         pages.append(placed([P, T], F32, "page2", 8))
         nc.gpsimd.memset(pages[2][:], 0.0)
         for nt in range(2):
-            half_tile(nt, 1)
+            make_unit(2 + nt, nt, 1)
             scatter(nt, HALF, J)
             store(nt)
         for nt in range(2, N_TILES):
             for h in range(2):
-                half_tile(nt, h)
+                make_unit(2 * nt + h, nt, h)
             scatter(nt, 0, J)
             store(nt)

@@ -38,7 +38,7 @@ def tile_list_rgg_none_kernel(
         psum = ctx.enter_context(tc.psum_pool(name="psum", bufs=1))
         words = ctx.enter_context(tc.tile_pool(name="words", bufs=1))
         bank_m = psum.tile([P, HALF], F32, name="bank_m")
-        turns = [psum.tile([P, HALF], F32, name="turn%d" % i) for i in range(2)]
+        turns = [psum.tile([P, HALF], F32, name="turn_%d" % i) for i in range(2)]
 
         src_list = keep.tile([P, J // LIST_ROWS], U16, name="src_list")
         dst_list = keep.tile([P, J // LIST_ROWS], U16, name="dst_list")
@@ -76,11 +76,11 @@ def tile_list_rgg_none_kernel(
         def placed(shape, dtype, name, kib):
             return late.tile(shape, dtype, name=name, offset=int(kib * 1024), align_bytes=64)
 
-        wb_bf = [placed([P, 256 * PACK], BF16, "wb_bf0", 16)]
+        wb_bf = [placed([P, 256 * PACK], BF16, "wb_bf0", 28)]
         wb_raw = [placed([P, PACK, N // 2], F32, "wb_raw0", 18)]
         wc_w = placed([P, 2 * N], U8, "wc_w", 0)
         wa_w = placed([P, 2 * N], U8, "wa_w", 1)
-        src_w = [placed([P, HALF], U32, "src_w%d" % h, 2 + 2 * h) for h in range(2)]
+        src_w = [placed([P, HALF], U32, "src_w0", 2)]
         dst_w = [placed([P, HALF], U32, "dst_w0", 6)]
         picked_src = placed([P, J], U8, "picked_src", 23)
         picked_dst = placed([P, HALF], U8, "picked_dst", 24)
@@ -116,14 +116,16 @@ def tile_list_rgg_none_kernel(
         def make_unit(unit, nt, h):
             bank_t, bank_g = turns[unit % 2], turns[(unit + 1) % 2]
             if unit == 0:
-                stage = placed([P, HALF], F32, "stage_first", 18)
+                bank_g = bank_m
+            if unit == 0:
+                stage = placed([P, HALF], F32, "stage_first", 16.5)
             elif unit == 1:
                 stage = placed([P, HALF], F32, "stage_second", 8)
             else:
                 stage = keep.tile([P, HALF], F32, name="stage", tag="stage%d" % (unit % 2), align_bytes=64)
             cols = slice(h * HALF, (h + 1) * HALF)
             chans = slice(nt * P, (nt + 1) * P)
-            acc = [bank_g if unit == 0 and i < 2 else bank_m for i in range(HALF // P)]
+            acc = [turns[1] if unit == 0 and i >= 2 else bank_m for i in range(HALF // P)]
             for i in range(HALF // P):
                 nc.tensor.matmul_mx(
                     out=acc[i][:, i * P : (i + 1) * P],
@@ -197,12 +199,13 @@ def tile_list_rgg_none_kernel(
         load_wb(1)
         gather(src_w[0][:], tab_w, src_list, 0, HALF)
         gather(dst_w[0][:], tab_w, dst_list, 0, HALF)
-        gather(src_w[1][:], tab_w, src_list, HALF, J)
         quantize_wb(0)
-        picked_late = placed([P, HALF], U8, "picked_late", 20)
-        dst_w.append(placed([P, HALF], U32, "dst_w1", 20.5))
+        picked_late = placed([P, HALF], U8, "picked_late", 18.5)
+        src_w.append(placed([P, HALF], U32, "src_w1", 19))
+        dst_w.append(placed([P, HALF], U32, "dst_w1", 21))
         gather(picked_late[:], tab_s, dst_list, HALF, J)
         move_scale_rows(dst_s[:, HALF:J], picked_late)
+        gather(src_w[1][:], tab_w, src_list, HALF, J)
         gather(dst_w[1][:], tab_w, dst_list, HALF, J)
         pages.append(words.tile([P, T], F32, name="page1", offset=0, align_bytes=64))
         nc.gpsimd.memset(pages[1][:], 0.0)

@@ -39,6 +39,7 @@ def tile_list_rgg_none_kernel(
         words = ctx.enter_context(tc.tile_pool(name="words", bufs=1))
         bank_m = psum.tile([P, HALF], F32, name="bank_m")
         turns = [psum.tile([P, HALF], F32, name="turn_%d" % i) for i in range(2)]
+        spare = [psum.tile([P, HALF], F32, name="spare_%d" % i) for i in range(2)]
 
         src_list = keep.tile([P, J // LIST_ROWS], U16, name="src_list")
         dst_list = keep.tile([P, J // LIST_ROWS], U16, name="dst_list")
@@ -80,6 +81,7 @@ def tile_list_rgg_none_kernel(
         wb_raw = [placed([P, PACK, N // 2], F32, "wb_raw0", 18)]
         wc_w = placed([P, 2 * N], U8, "wc_w", 0)
         wa_w = placed([P, 2 * N], U8, "wa_w", 1)
+        wa_rows = placed([P, N], U8, "wa_rows", 30)
         src_w = [placed([P, HALF], U32, "src_w0", 2)]
         dst_w = [placed([P, HALF], U32, "dst_w0", 6)]
         picked_src = placed([P, J], U8, "picked_src", 23)
@@ -117,6 +119,8 @@ def tile_list_rgg_none_kernel(
             bank_t, bank_g = turns[unit % 2], turns[(unit + 1) % 2]
             if unit == 0:
                 bank_g = bank_m
+            if unit == 1:
+                bank_t, bank_g = bank_m, spare[1]
             if unit == 0:
                 stage = placed([P, HALF], F32, "stage_first", 16.5)
             elif unit == 1:
@@ -126,6 +130,8 @@ def tile_list_rgg_none_kernel(
             cols = slice(h * HALF, (h + 1) * HALF)
             chans = slice(nt * P, (nt + 1) * P)
             acc = [turns[1] if unit == 0 and i >= 2 else bank_m for i in range(HALF // P)]
+            if unit == 1:
+                acc = [spare[0]] * (HALF // P)
             for i in range(HALF // P):
                 nc.tensor.matmul_mx(
                     out=acc[i][:, i * P : (i + 1) * P],
@@ -178,12 +184,12 @@ def tile_list_rgg_none_kernel(
         nc.scalar.activation(warm[:], warm_in[:], SIGMOID)
         nc.sync.dma_start(tab_w[:].bitcast(I32), tab_words[0].rearrange("p t i -> p (t i)").bitcast(I32))
         load_scale_rows(nc.sync, wc_s, wc_scales)
+        nc.sync.dma_start(wa_rows[FIRST_ROW:P].bitcast(I32), wa_scales[0].bitcast(I32))
         nc.sync.dma_start(wgo_rows[0:J_TILES, :], wgo[0, :].rearrange("(a b) -> a b", b=P))
         load_wb(0)
         nc.sync.dma_start(wc_w[:].bitcast(I32), wc_words[0].bitcast(I32))
         nc.sync.dma_start(wa_w[:].bitcast(I32), wa_words[0].bitcast(I32))
 
-        load_scale_rows(nc.gpsimd, wa_s, wa_scales)
         pages = [placed([P, T], F32, "page0", 32)]
         nc.gpsimd.memset(pages[0][:], 0.0)
 
@@ -195,6 +201,7 @@ def tile_list_rgg_none_kernel(
         move_scale_rows(src_s, picked_src)
         gather(picked_dst[:], tab_s, dst_list, 0, HALF)
         move_scale_rows(dst_s[:, 0:HALF], picked_dst)
+        move_scale_rows(wa_s, wa_rows)
         wb_raw.append(placed([P, PACK, N // 2], F32, "wb_raw1", 23))
         load_wb(1)
         gather(src_w[0][:], tab_w, src_list, 0, HALF)

@@ -57,8 +57,8 @@ def tile_list_rgg_none_kernel(
         eta = [keep.tile([P, J], F32, name="eta%d" % nt) for nt in range(N_TILES)]
         warm_in = keep.tile([P, 1], F32, name="warm_in")
         warm = keep.tile([P, 1], F32, name="warm")
-        src_s = planes[:, 0:J]
-        dst_s = planes[:, J : 2 * J]
+        src_s = [planes[:, h * J : h * J + HALF] for h in range(2)]
+        dst_s = [planes[:, h * J + HALF : (h + 1) * J] for h in range(2)]
 
         tab_w = words.tile([P, T], U32, name="tab_w", offset=0, align_bytes=64)
 
@@ -82,10 +82,10 @@ def tile_list_rgg_none_kernel(
         wc_w = placed([P, 2 * N], U8, "wc_w", 0)
         wa_w = placed([P, 2 * N], U8, "wa_w", 1)
         wa_rows = placed([P, N], U8, "wa_rows", 30)
-        src_w = [placed([P, HALF], U32, "src_w0", 2)]
+        src_all = placed([P, J], U32, "src_all", 2)
+        src_w = [src_all[:, 0:HALF], src_all[:, HALF:J]]
         dst_w = [placed([P, HALF], U32, "dst_w0", 6)]
-        picked_src = placed([P, J], U8, "picked_src", 23)
-        picked_dst = placed([P, HALF], U8, "picked_dst", 24)
+        picked = placed([P, J], U8, "picked", 24)
 
         def load_scale_rows(queue, plane, rows):
             for q in range(4):
@@ -136,7 +136,7 @@ def tile_list_rgg_none_kernel(
                 nc.tensor.matmul_mx(
                     out=acc[i][:, i * P : (i + 1) * P],
                     lhsT=src_w[h][:, i * P : (i + 1) * P].bitcast(FP8X4),
-                    lhsT_scale=src_s[:, h * HALF + i * P : h * HALF + (i + 1) * P],
+                    lhsT_scale=src_s[h][:, i * P : (i + 1) * P],
                     rhs=wc_w[:, 2 * nt * P : 2 * (nt + 1) * P].bitcast(FP4X4),
                     rhs_scale=wc_s[:, chans],
                     start=True,
@@ -155,7 +155,7 @@ def tile_list_rgg_none_kernel(
                 lhsT=wa_w[:, 2 * nt * P : 2 * (nt + 1) * P].bitcast(FP4X4),
                 lhsT_scale=wa_s[:, chans],
                 rhs=dst_w[h][:].bitcast(FP8X4),
-                rhs_scale=dst_s[:, cols],
+                rhs_scale=dst_s[h],
                 start=True,
                 stop=False,
             )
@@ -163,8 +163,8 @@ def tile_list_rgg_none_kernel(
                 out=bank_g[:],
                 lhsT=wb_w[:, chans].bitcast(FP8X4),
                 lhsT_scale=wb_s[:, chans],
-                rhs=src_w[h][:].bitcast(FP8X4),
-                rhs_scale=src_s[:, cols],
+                rhs=src_w[h].bitcast(FP8X4),
+                rhs_scale=src_s[h],
                 start=False,
                 stop=True,
             )
@@ -197,22 +197,20 @@ def tile_list_rgg_none_kernel(
         nc.scalar.copy(wgo_cols[:], turns[0][:, 0:J_TILES])
         round_wb(0)
 
-        gather(picked_src[:], tab_s, src_list, 0, J)
-        move_scale_rows(src_s, picked_src)
-        gather(picked_dst[:], tab_s, dst_list, 0, HALF)
-        move_scale_rows(dst_s[:, 0:HALF], picked_dst)
+        gather(picked[:, 0:HALF], tab_s, src_list, 0, HALF)
+        gather(picked[:, HALF:J], tab_s, dst_list, 0, HALF)
+        move_scale_rows(planes[:, 0:J], picked)
         move_scale_rows(wa_s, wa_rows)
-        wb_raw.append(placed([P, PACK, N // 2], F32, "wb_raw1", 23))
+        wb_raw.append(placed([P, PACK, N // 2], F32, "wb_raw1", 24))
         load_wb(1)
-        gather(src_w[0][:], tab_w, src_list, 0, HALF)
+        gather(src_all[:], tab_w, src_list, 0, J)
         gather(dst_w[0][:], tab_w, dst_list, 0, HALF)
         quantize_wb(0)
-        picked_late = placed([P, HALF], U8, "picked_late", 18.5)
-        src_w.append(placed([P, HALF], U32, "src_w1", 19))
-        dst_w.append(placed([P, HALF], U32, "dst_w1", 21))
-        gather(picked_late[:], tab_s, dst_list, HALF, J)
-        move_scale_rows(dst_s[:, HALF:J], picked_late)
-        gather(src_w[1][:], tab_w, src_list, HALF, J)
+        dst_w.append(placed([P, HALF], U32, "dst_w1", 19.5))
+        picked_late = placed([P, J], U8, "picked_late", 18.5)
+        gather(picked_late[:, 0:HALF], tab_s, src_list, HALF, J)
+        gather(picked_late[:, HALF:J], tab_s, dst_list, HALF, J)
+        move_scale_rows(planes[:, J : 2 * J], picked_late)
         gather(dst_w[1][:], tab_w, dst_list, HALF, J)
         pages.append(words.tile([P, T], F32, name="page1", offset=0, align_bytes=64))
         nc.gpsimd.memset(pages[1][:], 0.0)

@@ -84,7 +84,8 @@ def tile_list_rgg_none_kernel(
         wa_rows = placed([P, N], U8, "wa_rows", 30)
         src_all = placed([P, J], U32, "src_all", 2)
         src_w = [src_all[:, 0:HALF], src_all[:, HALF:J]]
-        dst_w = [placed([P, HALF], U32, "dst_w0", 6)]
+        dst_all = placed([P, J], U32, "dst_all", 40)
+        dst_w = [dst_all[:, 0:HALF], dst_all[:, HALF:J]]
         picked = placed([P, J], U8, "picked", 24)
 
         def load_scale_rows(queue, plane, rows):
@@ -154,7 +155,7 @@ def tile_list_rgg_none_kernel(
                 out=bank_g[:],
                 lhsT=wa_w[:, 2 * nt * P : 2 * (nt + 1) * P].bitcast(FP4X4),
                 lhsT_scale=wa_s[:, chans],
-                rhs=dst_w[h][:].bitcast(FP8X4),
+                rhs=dst_w[h].bitcast(FP8X4),
                 rhs_scale=dst_s[h],
                 start=True,
                 stop=False,
@@ -204,14 +205,12 @@ def tile_list_rgg_none_kernel(
         wb_raw.append(placed([P, PACK, N // 2], F32, "wb_raw1", 24))
         load_wb(1)
         gather(src_all[:], tab_w, src_list, 0, J)
-        gather(dst_w[0][:], tab_w, dst_list, 0, HALF)
+        gather(dst_all[:], tab_w, dst_list, 0, J)
         quantize_wb(0)
-        dst_w.append(placed([P, HALF], U32, "dst_w1", 19.5))
         picked_late = placed([P, J], U8, "picked_late", 18.5)
         gather(picked_late[:, 0:HALF], tab_s, src_list, HALF, J)
         gather(picked_late[:, HALF:J], tab_s, dst_list, HALF, J)
         move_scale_rows(planes[:, J : 2 * J], picked_late)
-        gather(dst_w[1][:], tab_w, dst_list, HALF, J)
         pages.append(words.tile([P, T], F32, name="page1", offset=0, align_bytes=64))
         nc.gpsimd.memset(pages[1][:], 0.0)
 

@@ -26,6 +26,7 @@ LIST_ROWS = 16
 QUAD = 32
 SCALE_ROWS = 16
 FIRST_ROW = P - SCALE_ROWS
+EARLY = 768
 
 
 def tile_list_rgg_none_kernel(
@@ -57,8 +58,11 @@ def tile_list_rgg_none_kernel(
         eta = [keep.tile([P, J], F32, name="eta%d" % nt) for nt in range(N_TILES)]
         warm_in = keep.tile([P, 1], F32, name="warm_in")
         warm = keep.tile([P, 1], F32, name="warm")
-        src_s = [planes[:, h * J : h * J + HALF] for h in range(2)]
-        dst_s = [planes[:, h * J + HALF : (h + 1) * J] for h in range(2)]
+        dst_s = [planes[:, EARLY : EARLY + HALF], planes[:, 2 * J - HALF : 2 * J]]
+
+        def src_s(lo, hi):
+            shift = 0 if lo < EARLY else HALF
+            return planes[:, lo + shift : hi + shift]
 
         tab_w = words.tile([P, T], U32, name="tab_w", offset=0, align_bytes=64)
 
@@ -86,7 +90,7 @@ def tile_list_rgg_none_kernel(
         src_w = [src_all[:, 0:HALF], src_all[:, HALF:J]]
         dst_all = placed([P, J], U32, "dst_all", 40)
         dst_w = [dst_all[:, 0:HALF], dst_all[:, HALF:J]]
-        picked = placed([P, J], U8, "picked", 24)
+        picked = placed([P, EARLY + HALF], U8, "picked", 24)
 
         def load_scale_rows(queue, plane, rows):
             for q in range(4):
@@ -137,7 +141,7 @@ def tile_list_rgg_none_kernel(
                 nc.tensor.matmul_mx(
                     out=acc[i][:, i * P : (i + 1) * P],
                     lhsT=src_w[h][:, i * P : (i + 1) * P].bitcast(FP8X4),
-                    lhsT_scale=src_s[h][:, i * P : (i + 1) * P],
+                    lhsT_scale=src_s(h * HALF + i * P, h * HALF + (i + 1) * P),
                     rhs=wc_w[:, 2 * nt * P : 2 * (nt + 1) * P].bitcast(FP4X4),
                     rhs_scale=wc_s[:, chans],
                     start=True,
@@ -160,15 +164,17 @@ def tile_list_rgg_none_kernel(
                 start=True,
                 stop=False,
             )
-            nc.tensor.matmul_mx(
-                out=bank_g[:],
-                lhsT=wb_w[:, chans].bitcast(FP8X4),
-                lhsT_scale=wb_s[:, chans],
-                rhs=src_w[h].bitcast(FP8X4),
-                rhs_scale=src_s[h],
-                start=False,
-                stop=True,
-            )
+            cuts = [0, HALF] if h == 0 else [0, EARLY - HALF, HALF]
+            for lo, hi in zip(cuts[:-1], cuts[1:]):
+                nc.tensor.matmul_mx(
+                    out=bank_g[:, lo:hi],
+                    lhsT=wb_w[:, chans].bitcast(FP8X4),
+                    lhsT_scale=wb_s[:, chans],
+                    rhs=src_w[h][:, lo:hi].bitcast(FP8X4),
+                    rhs_scale=src_s(h * HALF + lo, h * HALF + hi),
+                    start=False,
+                    stop=hi == HALF,
+                )
             nc.scalar.activation(eta[nt][:, cols], bank_g[:], SIGMOID)
 
         def scatter(nt, lo, hi):
@@ -198,19 +204,19 @@ def tile_list_rgg_none_kernel(
         nc.scalar.copy(wgo_cols[:], turns[0][:, 0:J_TILES])
         round_wb(0)
 
-        gather(picked[:, 0:HALF], tab_s, src_list, 0, HALF)
-        gather(picked[:, HALF:J], tab_s, dst_list, 0, HALF)
-        move_scale_rows(planes[:, 0:J], picked)
+        gather(picked[:, 0:EARLY], tab_s, src_list, 0, EARLY)
+        gather(picked[:, EARLY : EARLY + HALF], tab_s, dst_list, 0, HALF)
+        move_scale_rows(planes[:, 0 : EARLY + HALF], picked)
         move_scale_rows(wa_s, wa_rows)
         wb_raw.append(placed([P, PACK, N // 2], F32, "wb_raw1", 24))
         load_wb(1)
         gather(src_all[:], tab_w, src_list, 0, J)
         gather(dst_all[:], tab_w, dst_list, 0, J)
         quantize_wb(0)
-        picked_late = placed([P, J], U8, "picked_late", 18.5)
-        gather(picked_late[:, 0:HALF], tab_s, src_list, HALF, J)
-        gather(picked_late[:, HALF:J], tab_s, dst_list, HALF, J)
-        move_scale_rows(planes[:, J : 2 * J], picked_late)
+        picked_late = placed([P, J - EARLY + HALF], U8, "picked_late", 18.5)
+        gather(picked_late[:, 0 : J - EARLY], tab_s, src_list, EARLY, J)
+        gather(picked_late[:, J - EARLY : J - EARLY + HALF], tab_s, dst_list, HALF, J)
+        move_scale_rows(planes[:, EARLY + HALF : 2 * J], picked_late)
         pages.append(words.tile([P, T], F32, name="page1", offset=0, align_bytes=64))
         nc.gpsimd.memset(pages[1][:], 0.0)
 

@@ -81,7 +81,7 @@ def tile_list_rgg_none_kernel(
         def placed(shape, dtype, name, kib):
             return late.tile(shape, dtype, name=name, offset=int(kib * 1024), align_bytes=64)
 
-        wb_bf = [placed([P, 256 * PACK], BF16, "wb_bf0", 28)]
+        wb_bf = [placed([P, 256 * PACK], BF16, "wb_bf0", 44)]
         wb_raw = [placed([P, PACK, N // 2], F32, "wb_raw0", 18)]
         wc_w = placed([P, 2 * N], U8, "wc_w", 0)
         wa_w = placed([P, 2 * N], U8, "wa_w", 1)
@@ -202,7 +202,14 @@ def tile_list_rgg_none_kernel(
 
         nc.tensor.transpose(turns[0][:, 0:P], wgo_rows[:], ident[:])
         nc.scalar.copy(wgo_cols[:], turns[0][:, 0:J_TILES])
-        round_wb(0)
+        nc.gpsimd.tensor_scalar(
+            wb_bf[0][:].rearrange("p (c t) -> p c t", t=PACK),
+            wb_raw[0][:].rearrange("p t c -> p c t"),
+            1.0,
+            0.0,
+            MULT,
+            mybir.AluOpType.add,
+        )
 
         gather(picked[:, 0:EARLY], tab_s, src_list, 0, EARLY)
         gather(picked[:, EARLY : EARLY + HALF], tab_s, dst_list, 0, HALF)
@@ -217,7 +224,7 @@ def tile_list_rgg_none_kernel(
         gather(picked_late[:, 0 : J - EARLY], tab_s, src_list, EARLY, J)
         gather(picked_late[:, J - EARLY : J - EARLY + HALF], tab_s, dst_list, HALF, J)
         move_scale_rows(planes[:, EARLY + HALF : 2 * J], picked_late)
-        pages.append(words.tile([P, T], F32, name="page1", offset=0, align_bytes=64))
+        pages.append(placed([P, T], F32, "page1", 44))
         nc.gpsimd.memset(pages[1][:], 0.0)
 
         for nt in range(2):

@@ -27,6 +27,8 @@ QUAD = 32
 SCALE_ROWS = 16
 FIRST_ROW = P - SCALE_ROWS
 EARLY = 768
+PIECE = 256
+ROUND_AFTER = 4
 
 
 def tile_list_rgg_none_kernel(
@@ -38,9 +40,7 @@ def tile_list_rgg_none_kernel(
         keep = ctx.enter_context(tc.tile_pool(name="keep", bufs=1))
         psum = ctx.enter_context(tc.psum_pool(name="psum", bufs=1))
         words = ctx.enter_context(tc.tile_pool(name="words", bufs=1))
-        bank_m = psum.tile([P, HALF], F32, name="bank_m")
-        turns = [psum.tile([P, HALF], F32, name="turn_%d" % i) for i in range(2)]
-        spare = [psum.tile([P, HALF], F32, name="spare_%d" % i) for i in range(2)]
+        banks = [psum.tile([P, HALF], F32, name="bank_%d" % i) for i in range(5)]
 
         src_list = keep.tile([P, J // LIST_ROWS], U16, name="src_list")
         dst_list = keep.tile([P, J // LIST_ROWS], U16, name="dst_list")
@@ -58,10 +58,13 @@ def tile_list_rgg_none_kernel(
         eta = [keep.tile([P, J], F32, name="eta%d" % nt) for nt in range(N_TILES)]
         warm_in = keep.tile([P, 1], F32, name="warm_in")
         warm = keep.tile([P, 1], F32, name="warm")
-        dst_s = [planes[:, EARLY : EARLY + HALF], planes[:, 2 * J - HALF : 2 * J]]
 
         def src_s(lo, hi):
             shift = 0 if lo < EARLY else HALF
+            return planes[:, lo + shift : hi + shift]
+
+        def dst_s(lo, hi):
+            shift = EARLY if lo < HALF else J
             return planes[:, lo + shift : hi + shift]
 
         tab_w = words.tile([P, T], U32, name="tab_w", offset=0, align_bytes=64)
@@ -85,11 +88,8 @@ def tile_list_rgg_none_kernel(
         wb_raw = [placed([P, PACK, N // 2], F32, "wb_raw0", 18)]
         wc_w = placed([P, 2 * N], U8, "wc_w", 0)
         wa_w = placed([P, 2 * N], U8, "wa_w", 1)
-        wa_rows = placed([P, N], U8, "wa_rows", 30)
-        src_all = placed([P, J], U32, "src_all", 2)
-        src_w = [src_all[:, 0:HALF], src_all[:, HALF:J]]
-        dst_all = placed([P, J], U32, "dst_all", 40)
-        dst_w = [dst_all[:, 0:HALF], dst_all[:, HALF:J]]
+        src_runs = [(0, placed([P, HALF], U32, "src_first", 2))]
+        dst_runs = [(0, placed([P, HALF], U32, "dst_first", 4))]
         picked = placed([P, EARLY + HALF], U8, "picked", 24)
 
         def load_scale_rows(queue, plane, rows):
@@ -120,62 +120,63 @@ def tile_list_rgg_none_kernel(
             cols = slice(i * 256, (i + 1) * 256)
             nc.vector.quantize_mx(out=wb_w[:, cols].bitcast(FP8X4), scales=wb_s[:, cols], in_=wb_bf[i][:])
 
-        def make_unit(unit, nt, h):
-            bank_t, bank_g = turns[unit % 2], turns[(unit + 1) % 2]
-            if unit == 0:
-                bank_g = bank_m
-            if unit == 1:
-                bank_t, bank_g = bank_m, spare[1]
-            if unit == 0:
-                stage = placed([P, HALF], F32, "stage_first", 16.5)
-            elif unit == 1:
-                stage = placed([P, HALF], F32, "stage_second", 8)
-            else:
-                stage = keep.tile([P, HALF], F32, name="stage", tag="stage%d" % (unit % 2), align_bytes=64)
-            cols = slice(h * HALF, (h + 1) * HALF)
+        def words_of(runs, lo, hi):
+            first, run = [entry for entry in runs if entry[0] <= lo][-1]
+            return run[:, lo - first : hi - first].bitcast(FP8X4)
+
+        def gather_late(runs, lst, lo, kib):
+            run = placed([P, PIECE], U32, "late_words_%d" % int(kib), kib)
+            runs.append((lo, run))
+            gather(run[:], tab_w, lst, lo, lo + PIECE)
+
+        def make_unit(unit, nt, lo, hi, stage):
+            bank_m = banks[2 * (unit % 2)]
+            bank_g = banks[2] if unit == 0 else bank_m
+            bank_t = banks[0] if unit == 1 else banks[1]
+            if unit in (5, 6):
+                bank_t = banks[unit - 2]
+            if unit in (8, 9):
+                bank_m = bank_g = banks[unit - 5]
             chans = slice(nt * P, (nt + 1) * P)
-            acc = [turns[1] if unit == 0 and i >= 2 else bank_m for i in range(HALF // P)]
-            if unit == 1:
-                acc = [spare[0]] * (HALF // P)
-            for i in range(HALF // P):
+            blocks = [(i * P, (i + 1) * P) for i in range((hi - lo) // P)]
+            for a, b in blocks:
                 nc.tensor.matmul_mx(
-                    out=acc[i][:, i * P : (i + 1) * P],
-                    lhsT=src_w[h][:, i * P : (i + 1) * P].bitcast(FP8X4),
-                    lhsT_scale=src_s(h * HALF + i * P, h * HALF + (i + 1) * P),
+                    out=bank_m[:, a:b],
+                    lhsT=words_of(src_runs, lo + a, lo + b),
+                    lhsT_scale=src_s(lo + a, lo + b),
                     rhs=wc_w[:, 2 * nt * P : 2 * (nt + 1) * P].bitcast(FP4X4),
                     rhs_scale=wc_s[:, chans],
                     start=True,
                     stop=True,
                 )
-            for i in range(HALF // P):
-                jt = h * (HALF // P) + i
-                nc.scalar.activation(
-                    stage[:, i * P : (i + 1) * P], acc[i][:, i * P : (i + 1) * P], COPY, scale=wgo_cols[:, jt : jt + 1]
-                )
-            for i in range(HALF // P):
-                nc.tensor.transpose(bank_t[:, i * P : (i + 1) * P], stage[:, i * P : (i + 1) * P], ident[:])
-            nc.scalar.copy(msw[nt][:, cols], bank_t[:])
-            nc.tensor.matmul_mx(
-                out=bank_g[:],
-                lhsT=wa_w[:, 2 * nt * P : 2 * (nt + 1) * P].bitcast(FP4X4),
-                lhsT_scale=wa_s[:, chans],
-                rhs=dst_w[h].bitcast(FP8X4),
-                rhs_scale=dst_s[h],
-                start=True,
-                stop=False,
-            )
-            cuts = [0, HALF] if h == 0 else [0, EARLY - HALF, HALF]
-            for lo, hi in zip(cuts[:-1], cuts[1:]):
+            for a, b in blocks:
+                jt = (lo + a) // P
+                nc.scalar.activation(stage[:, a:b], bank_m[:, a:b], COPY, scale=wgo_cols[:, jt : jt + 1])
+            for a, b in blocks:
+                nc.tensor.transpose(bank_t[:, a:b], stage[:, a:b], ident[:])
+            nc.scalar.copy(msw[nt][:, lo:hi], bank_t[:, 0 : hi - lo])
+            runs = [(lo, hi)] if lo < HALF else [(a, a + PIECE) for a in range(lo, hi, PIECE)]
+            for a, b in runs:
                 nc.tensor.matmul_mx(
-                    out=bank_g[:, lo:hi],
+                    out=bank_g[:, a - lo : b - lo],
+                    lhsT=wa_w[:, 2 * nt * P : 2 * (nt + 1) * P].bitcast(FP4X4),
+                    lhsT_scale=wa_s[:, chans],
+                    rhs=words_of(dst_runs, a, b),
+                    rhs_scale=dst_s(a, b),
+                    start=a == lo,
+                    stop=False,
+                )
+            for a, b in runs:
+                nc.tensor.matmul_mx(
+                    out=bank_g[:, a - lo : b - lo],
                     lhsT=wb_w[:, chans].bitcast(FP8X4),
                     lhsT_scale=wb_s[:, chans],
-                    rhs=src_w[h][:, lo:hi].bitcast(FP8X4),
-                    rhs_scale=src_s(h * HALF + lo, h * HALF + hi),
+                    rhs=words_of(src_runs, a, b),
+                    rhs_scale=src_s(a, b),
                     start=False,
-                    stop=hi == HALF,
+                    stop=b == hi,
                 )
-            nc.scalar.activation(eta[nt][:, cols], bank_g[:], SIGMOID)
+            nc.scalar.activation(eta[nt][:, lo:hi], bank_g[:, 0 : hi - lo], SIGMOID)
 
         def scatter(nt, lo, hi):
             page = pages[nt % 3]
@@ -191,56 +192,54 @@ def tile_list_rgg_none_kernel(
         nc.scalar.activation(warm[:], warm_in[:], SIGMOID)
         nc.sync.dma_start(tab_w[:].bitcast(I32), tab_words[0].rearrange("p t i -> p (t i)").bitcast(I32))
         load_scale_rows(nc.sync, wc_s, wc_scales)
-        nc.sync.dma_start(wa_rows[FIRST_ROW:P].bitcast(I32), wa_scales[0].bitcast(I32))
+        load_scale_rows(nc.gpsimd, wa_s, wa_scales)
         nc.sync.dma_start(wgo_rows[0:J_TILES, :], wgo[0, :].rearrange("(a b) -> a b", b=P))
         load_wb(0)
         nc.sync.dma_start(wc_w[:].bitcast(I32), wc_words[0].bitcast(I32))
         nc.sync.dma_start(wa_w[:].bitcast(I32), wa_words[0].bitcast(I32))
 
-        pages = [placed([P, T], F32, "page0", 32)]
+        pages = [placed([P, T], F32, "page0", 70)]
         nc.gpsimd.memset(pages[0][:], 0.0)
 
-        nc.tensor.transpose(turns[0][:, 0:P], wgo_rows[:], ident[:])
-        nc.scalar.copy(wgo_cols[:], turns[0][:, 0:J_TILES])
-        nc.gpsimd.tensor_scalar(
-            wb_bf[0][:].rearrange("p (c t) -> p c t", t=PACK),
-            wb_raw[0][:].rearrange("p t c -> p c t"),
-            1.0,
-            0.0,
-            MULT,
-            mybir.AluOpType.add,
-        )
+        nc.tensor.transpose(banks[1][:, 0:P], wgo_rows[:], ident[:])
+        nc.scalar.copy(wgo_cols[:], banks[1][:, 0:J_TILES])
+        round_wb(0)
 
         gather(picked[:, 0:EARLY], tab_s, src_list, 0, EARLY)
         gather(picked[:, EARLY : EARLY + HALF], tab_s, dst_list, 0, HALF)
         move_scale_rows(planes[:, 0 : EARLY + HALF], picked)
-        move_scale_rows(wa_s, wa_rows)
         wb_raw.append(placed([P, PACK, N // 2], F32, "wb_raw1", 24))
         load_wb(1)
-        gather(src_all[:], tab_w, src_list, 0, J)
-        gather(dst_all[:], tab_w, dst_list, 0, J)
+        gather(src_runs[0][1][:], tab_w, src_list, 0, HALF)
+        gather(dst_runs[0][1][:], tab_w, dst_list, 0, HALF)
         quantize_wb(0)
         picked_late = placed([P, J - EARLY + HALF], U8, "picked_late", 18.5)
         gather(picked_late[:, 0 : J - EARLY], tab_s, src_list, EARLY, J)
         gather(picked_late[:, J - EARLY : J - EARLY + HALF], tab_s, dst_list, HALF, J)
         move_scale_rows(planes[:, EARLY + HALF : 2 * J], picked_late)
-        pages.append(placed([P, T], F32, "page1", 44))
-        nc.gpsimd.memset(pages[1][:], 0.0)
+        for i in (1, 2):
+            pages.append(placed([P, T], F32, "page%d" % i, 29 + 8 * i))
+            nc.gpsimd.memset(pages[i][:], 0.0)
 
-        for nt in range(2):
-            make_unit(nt, nt, 0)
-            scatter(nt, 0, HALF)
-        wb_bf.append(placed([P, 256 * PACK], BF16, "wb_bf1", 8))
-        round_wb(1)
-        quantize_wb(1)
-        pages.append(placed([P, T], F32, "page2", 8))
-        nc.gpsimd.memset(pages[2][:], 0.0)
-        for nt in range(2):
-            make_unit(2 + nt, nt, 1)
-            scatter(nt, HALF, J)
-            store(nt)
+        late_runs = [
+            (runs, lst, lo) for lo in range(HALF, J, PIECE) for runs, lst in ((src_runs, src_list), (dst_runs, dst_list))
+        ]
+        for unit in range(2 * J // PIECE):
+            nt, lo = unit % 2, unit // 2 * PIECE
+            kib = 17.5 if unit == 0 else 7.5 if unit == ROUND_AFTER else 27.5 if unit == ROUND_AFTER + 2 else 52 + 2 * unit
+            make_unit(unit, nt, lo, lo + PIECE, placed([P, PIECE], F32, "stage_%d" % unit, kib))
+            if 1 <= unit <= len(late_runs):
+                gather_late(*late_runs[unit - 1], kib - 0.75)
+            if unit == ROUND_AFTER:
+                wb_bf.append(placed([P, 256 * PACK], BF16, "wb_bf1", 8))
+                round_wb(1)
+                quantize_wb(1)
+            scatter(nt, lo, lo + PIECE)
+            if lo + PIECE == J:
+                store(nt)
+        stages = [keep.tile([P, HALF], F32, name="stage_wide%d" % h, align_bytes=64) for h in range(2)]
         for nt in range(2, N_TILES):
             for h in range(2):
-                make_unit(2 * nt + h, nt, h)
+                make_unit(2 * nt + 4 + h, nt, h * HALF, (h + 1) * HALF, stages[h])
             scatter(nt, 0, J)
             store(nt)

@@ -26,9 +26,9 @@ LIST_ROWS = 16
 QUAD = 32
 SCALE_ROWS = 16
 FIRST_ROW = P - SCALE_ROWS
-EARLY = 768
+EARLY = 640
+LATE = J - EARLY
 PIECE = 256
-ROUND_AFTER = 4
 
 
 def tile_list_rgg_none_kernel(
@@ -40,7 +40,7 @@ def tile_list_rgg_none_kernel(
         keep = ctx.enter_context(tc.tile_pool(name="keep", bufs=1))
         psum = ctx.enter_context(tc.psum_pool(name="psum", bufs=1))
         words = ctx.enter_context(tc.tile_pool(name="words", bufs=1))
-        banks = [psum.tile([P, HALF], F32, name="bank_%d" % i) for i in range(5)]
+        banks = [psum.tile([P, HALF], F32, name="bank_%d" % i) for i in range(6)]
 
         src_list = keep.tile([P, J // LIST_ROWS], U16, name="src_list")
         dst_list = keep.tile([P, J // LIST_ROWS], U16, name="dst_list")
@@ -49,8 +49,8 @@ def tile_list_rgg_none_kernel(
         w_s = keep.tile([P, 2 * N], U8, name="w_s", align_bytes=64)
         wc_s = w_s[:, 0:N]
         wa_s = w_s[:, N : 2 * N]
-        wb_w = keep.tile([P, N], U32, name="wb_w", align_bytes=64)
-        wb_s = keep.tile([P, N], U8, name="wb_s", align_bytes=64)
+        wb_w = [keep.tile([P, N // 2], U32, name="wb_w%d" % i, align_bytes=64) for i in range(2)]
+        wb_s = [keep.tile([P, N // 2], U8, name="wb_s%d" % i, align_bytes=64) for i in range(2)]
         ident = keep.tile([P, P], F32, name="ident")
         wgo_rows = keep.tile([P, P], F32, name="wgo_rows")
         wgo_cols = keep.tile([P, J_TILES], F32, name="wgo_cols")
@@ -60,11 +60,11 @@ def tile_list_rgg_none_kernel(
         warm = keep.tile([P, 1], F32, name="warm")
 
         def src_s(lo, hi):
-            shift = 0 if lo < EARLY else HALF
+            shift = 0 if lo < EARLY else EARLY
             return planes[:, lo + shift : hi + shift]
 
         def dst_s(lo, hi):
-            shift = EARLY if lo < HALF else J
+            shift = EARLY if lo < EARLY else J
             return planes[:, lo + shift : hi + shift]
 
         tab_w = words.tile([P, T], U32, name="tab_w", offset=0, align_bytes=64)
@@ -88,18 +88,18 @@ def tile_list_rgg_none_kernel(
         wb_raw = [placed([P, PACK, N // 2], F32, "wb_raw0", 18)]
         wc_w = placed([P, 2 * N], U8, "wc_w", 0)
         wa_w = placed([P, 2 * N], U8, "wa_w", 1)
-        src_runs = [(0, placed([P, HALF], U32, "src_first", 2))]
-        dst_runs = [(0, placed([P, HALF], U32, "dst_first", 4))]
-        picked = placed([P, EARLY + HALF], U8, "picked", 24)
+        src_runs = [(0, placed([P, EARLY], U32, "src_first", 2))]
+        dst_runs = [(0, placed([P, EARLY], U32, "dst_first", 5))]
+        picked = placed([P, 2 * EARLY], U8, "picked", 24)
 
         def load_scale_rows(queue, plane, rows):
             for q in range(4):
                 queue.dma_start(plane[QUAD * q : QUAD * q + 4].bitcast(I32), rows[0, 4 * q : 4 * q + 4, :].bitcast(I32))
 
-        def move_scale_rows(plane, rows):
+        def move_scale_rows(queue, plane, rows):
             for q in range(4):
                 lo = FIRST_ROW + 4 * q
-                nc.sync.dma_start(plane[QUAD * q : QUAD * q + 4].bitcast(I32), rows[lo : lo + 4].bitcast(I32))
+                queue.dma_start(plane[QUAD * q : QUAD * q + 4].bitcast(I32), rows[lo : lo + 4].bitcast(I32))
 
         def load_wb(i):
             nc.sync.dma_start(wb_raw[i][:], wb.rearrange("(p t) n -> p t n", t=PACK)[:, :, i * 256 : (i + 1) * 256])
@@ -117,27 +117,29 @@ def tile_list_rgg_none_kernel(
             )
 
         def quantize_wb(i):
-            cols = slice(i * 256, (i + 1) * 256)
-            nc.vector.quantize_mx(out=wb_w[:, cols].bitcast(FP8X4), scales=wb_s[:, cols], in_=wb_bf[i][:])
+            nc.vector.quantize_mx(out=wb_w[i][:].bitcast(FP8X4), scales=wb_s[i][:], in_=wb_bf[i][:])
 
         def words_of(runs, lo, hi):
             first, run = [entry for entry in runs if entry[0] <= lo][-1]
             return run[:, lo - first : hi - first].bitcast(FP8X4)
 
-        def gather_late(runs, lst, lo, kib):
-            run = placed([P, PIECE], U32, "late_words_%d" % int(kib), kib)
-            runs.append((lo, run))
-            gather(run[:], tab_w, lst, lo, lo + PIECE)
+        def gather_late(runs, lst, name, kib):
+            run = placed([P, LATE], U32, name, kib)
+            runs.append((EARLY, run))
+            gather(run[:], tab_w, lst, EARLY, J)
 
-        def make_unit(unit, nt, lo, hi, stage):
-            bank_m = banks[2 * (unit % 2)]
-            bank_g = banks[2] if unit == 0 else bank_m
-            bank_t = banks[0] if unit == 1 else banks[1]
-            if unit in (5, 6):
-                bank_t = banks[unit - 2]
-            if unit in (8, 9):
-                bank_m = bank_g = banks[unit - 5]
+        def widths(lo, hi):
+            runs = []
+            for n in (HALF, 2 * P, P):
+                if hi - lo >= n:
+                    runs.append((lo, lo + n))
+                    lo = lo + n
+            return runs
+
+        def make_unit(nt, lo, hi, stage, sums, turned, gate):
+            bank_m, bank_t, bank_g = banks[sums], banks[turned], banks[gate]
             chans = slice(nt * P, (nt + 1) * P)
+            pair = slice(nt % 2 * P, (nt % 2 + 1) * P)
             blocks = [(i * P, (i + 1) * P) for i in range((hi - lo) // P)]
             for a, b in blocks:
                 nc.tensor.matmul_mx(
@@ -155,7 +157,7 @@ def tile_list_rgg_none_kernel(
             for a, b in blocks:
                 nc.tensor.transpose(bank_t[:, a:b], stage[:, a:b], ident[:])
             nc.scalar.copy(msw[nt][:, lo:hi], bank_t[:, 0 : hi - lo])
-            runs = [(lo, hi)] if lo < HALF else [(a, a + PIECE) for a in range(lo, hi, PIECE)]
+            runs = widths(lo, min(hi, EARLY)) + widths(max(lo, EARLY), hi)
             for a, b in runs:
                 nc.tensor.matmul_mx(
                     out=bank_g[:, a - lo : b - lo],
@@ -169,8 +171,8 @@ def tile_list_rgg_none_kernel(
             for a, b in runs:
                 nc.tensor.matmul_mx(
                     out=bank_g[:, a - lo : b - lo],
-                    lhsT=wb_w[:, chans].bitcast(FP8X4),
-                    lhsT_scale=wb_s[:, chans],
+                    lhsT=wb_w[nt // 2][:, pair].bitcast(FP8X4),
+                    lhsT_scale=wb_s[nt // 2][:, pair],
                     rhs=words_of(src_runs, a, b),
                     rhs_scale=src_s(a, b),
                     start=False,
@@ -206,40 +208,46 @@ def tile_list_rgg_none_kernel(
         round_wb(0)
 
         gather(picked[:, 0:EARLY], tab_s, src_list, 0, EARLY)
-        gather(picked[:, EARLY : EARLY + HALF], tab_s, dst_list, 0, HALF)
-        move_scale_rows(planes[:, 0 : EARLY + HALF], picked)
+        gather(picked[:, EARLY : 2 * EARLY], tab_s, dst_list, 0, EARLY)
+        move_scale_rows(nc.scalar, planes[:, 0 : 2 * EARLY], picked)
         wb_raw.append(placed([P, PACK, N // 2], F32, "wb_raw1", 24))
         load_wb(1)
-        gather(src_runs[0][1][:], tab_w, src_list, 0, HALF)
-        gather(dst_runs[0][1][:], tab_w, dst_list, 0, HALF)
+        gather(src_runs[0][1][:], tab_w, src_list, 0, EARLY)
+        gather(dst_runs[0][1][:], tab_w, dst_list, 0, EARLY)
         quantize_wb(0)
-        picked_late = placed([P, J - EARLY + HALF], U8, "picked_late", 18.5)
-        gather(picked_late[:, 0 : J - EARLY], tab_s, src_list, EARLY, J)
-        gather(picked_late[:, J - EARLY : J - EARLY + HALF], tab_s, dst_list, HALF, J)
-        move_scale_rows(planes[:, EARLY + HALF : 2 * J], picked_late)
+        picked_late = placed([P, 2 * LATE], U8, "picked_late", 18.5)
+        gather(picked_late[:, 0:LATE], tab_s, src_list, EARLY, J)
+        gather(picked_late[:, LATE : 2 * LATE], tab_s, dst_list, EARLY, J)
+        move_scale_rows(nc.sync, planes[:, 2 * EARLY : 2 * J], picked_late)
         for i in (1, 2):
             pages.append(placed([P, T], F32, "page%d" % i, 29 + 8 * i))
             nc.gpsimd.memset(pages[i][:], 0.0)
 
-        late_runs = [
-            (runs, lst, lo) for lo in range(HALF, J, PIECE) for runs, lst in ((src_runs, src_list), (dst_runs, dst_list))
-        ]
-        for unit in range(2 * J // PIECE):
-            nt, lo = unit % 2, unit // 2 * PIECE
-            kib = 17.5 if unit == 0 else 7.5 if unit == ROUND_AFTER else 27.5 if unit == ROUND_AFTER + 2 else 52 + 2 * unit
-            make_unit(unit, nt, lo, lo + PIECE, placed([P, PIECE], F32, "stage_%d" % unit, kib))
-            if 1 <= unit <= len(late_runs):
-                gather_late(*late_runs[unit - 1], kib - 0.75)
-            if unit == ROUND_AFTER:
-                wb_bf.append(placed([P, 256 * PACK], BF16, "wb_bf1", 8))
-                round_wb(1)
-                quantize_wb(1)
-            scatter(nt, lo, lo + PIECE)
-            if lo + PIECE == J:
-                store(nt)
+        def staged(name, width, kib):
+            return placed([P, width], F32, name, kib)
+
+        make_unit(0, 0, PIECE, staged("stage_0", PIECE, 14), 0, 1, 2)
+        scatter(0, 0, PIECE)
+        make_unit(1, 0, PIECE, staged("stage_1", PIECE, 54), 3, 2, 3)
+        gather_late(src_runs, src_list, "src_late", 54)
+        scatter(1, 0, PIECE)
+        make_unit(0, PIECE, EARLY, staged("stage_2", LATE, 56), 2, 4, 2)
+        gather_late(dst_runs, dst_list, "dst_late", 56)
+        scatter(0, PIECE, EARLY)
+        make_unit(1, PIECE, EARLY, staged("stage_3", LATE, 58), 3, 4, 3)
+        wb_bf.append(placed([P, 256 * PACK], BF16, "wb_bf1", 58))
+        round_wb(1)
+        quantize_wb(1)
+        scatter(1, PIECE, EARLY)
+        make_unit(0, EARLY, J, staged("stage_4", LATE, 27), 4, 1, 4)
+        scatter(0, EARLY, J)
+        store(0)
+        make_unit(1, EARLY, J, staged("stage_5", LATE, 60), 2, 1, 2)
+        scatter(1, EARLY, J)
+        store(1)
         stages = [keep.tile([P, HALF], F32, name="stage_wide%d" % h, align_bytes=64) for h in range(2)]
         for nt in range(2, N_TILES):
             for h in range(2):
-                make_unit(2 * nt + 4 + h, nt, h * HALF, (h + 1) * HALF, stages[h])
+                make_unit(nt, h * HALF, (h + 1) * HALF, stages[h], 3 + h, 5 * h, 3 + h)
             scatter(nt, 0, J)
             store(nt)

@@ -46,9 +46,7 @@ def tile_list_rgg_none_kernel(
         dst_list = keep.tile([P, J // LIST_ROWS], U16, name="dst_list")
         tab_s = keep.tile([P, T], U8, name="tab_s", align_bytes=64)
         planes = keep.tile([P, 2 * J], U8, name="planes", align_bytes=64)
-        w_s = keep.tile([P, 2 * N], U8, name="w_s", align_bytes=64)
-        wc_s = w_s[:, 0:N]
-        wa_s = w_s[:, N : 2 * N]
+        wc_s = keep.tile([P, N], U8, name="wc_s", align_bytes=64)
         wb_w = [keep.tile([P, N // 2], U32, name="wb_w%d" % i, align_bytes=64) for i in range(2)]
         wb_s = [keep.tile([P, N // 2], U8, name="wb_s%d" % i, align_bytes=64) for i in range(2)]
         ident = keep.tile([P, P], F32, name="ident")
@@ -69,7 +67,7 @@ def tile_list_rgg_none_kernel(
 
         tab_w = words.tile([P, T], U32, name="tab_w", offset=0, align_bytes=64)
 
-        nc.vector.memset(w_s[:].bitcast(I32), 0)
+        nc.vector.memset(wc_s[:].bitcast(I32), 0)
         nc.vector.memset(warm_in[:], 0.0)
         nc.vector.memset(tab_s[0:FIRST_ROW].bitcast(I32), 0)
         nc.vector.memset(wgo_rows[:], 0.0)
@@ -194,7 +192,6 @@ def tile_list_rgg_none_kernel(
         nc.scalar.activation(warm[:], warm_in[:], SIGMOID)
         nc.sync.dma_start(tab_w[:].bitcast(I32), tab_words[0].rearrange("p t i -> p (t i)").bitcast(I32))
         load_scale_rows(nc.sync, wc_s, wc_scales)
-        load_scale_rows(nc.gpsimd, wa_s, wa_scales)
         nc.sync.dma_start(wgo_rows[0:J_TILES, :], wgo[0, :].rearrange("(a b) -> a b", b=P))
         load_wb(0)
         nc.sync.dma_start(wc_w[:].bitcast(I32), wc_words[0].bitcast(I32))
@@ -202,16 +199,24 @@ def tile_list_rgg_none_kernel(
 
         pages = [placed([P, T], F32, "page0", 70)]
         nc.gpsimd.memset(pages[0][:], 0.0)
+        wa_s = placed([P, N], U8, "wa_s", 8)
+        nc.gpsimd.memset(wa_s[:].bitcast(I32), 0)
 
         nc.tensor.transpose(banks[1][:, 0:P], wgo_rows[:], ident[:])
         nc.scalar.copy(wgo_cols[:], banks[1][:, 0:J_TILES])
-        round_wb(0)
+        nc.gpsimd.tensor_scalar(
+            wb_bf[0][:].rearrange("p (c t) -> p c t", t=PACK),
+            wb_raw[0][:].rearrange("p t c -> p c t"),
+            1.0,
+            0.0,
+            MULT,
+            mybir.AluOpType.add,
+        )
 
         gather(picked[:, 0:EARLY], tab_s, src_list, 0, EARLY)
         gather(picked[:, EARLY : 2 * EARLY], tab_s, dst_list, 0, EARLY)
-        move_scale_rows(nc.scalar, planes[:, 0 : 2 * EARLY], picked)
-        wb_raw.append(placed([P, PACK, N // 2], F32, "wb_raw1", 24))
-        load_wb(1)
+        move_scale_rows(nc.sync, planes[:, 0 : 2 * EARLY], picked)
+        load_scale_rows(nc.sync, wa_s, wa_scales)
         gather(src_runs[0][1][:], tab_w, src_list, 0, EARLY)
         gather(dst_runs[0][1][:], tab_w, dst_list, 0, EARLY)
         quantize_wb(0)
@@ -228,6 +233,8 @@ def tile_list_rgg_none_kernel(
 
         make_unit(0, 0, PIECE, staged("stage_0", PIECE, 14), 0, 1, 2)
         scatter(0, 0, PIECE)
+        wb_raw.append(placed([P, PACK, N // 2], F32, "wb_raw1", 14))
+        load_wb(1)
         make_unit(1, 0, PIECE, staged("stage_1", PIECE, 54), 3, 2, 3)
         gather_late(src_runs, src_list, "src_late", 54)
         scatter(1, 0, PIECE)
@@ -239,7 +246,7 @@ def tile_list_rgg_none_kernel(
         round_wb(1)
         quantize_wb(1)
         scatter(1, PIECE, EARLY)
-        make_unit(0, EARLY, J, staged("stage_4", LATE, 27), 4, 1, 4)
+        make_unit(0, EARLY, J, staged("stage_4", LATE, 16), 4, 1, 4)
         scatter(0, EARLY, J)
         store(0)
         make_unit(1, EARLY, J, staged("stage_5", LATE, 60), 2, 1, 2)

@@ -86,8 +86,8 @@ def tile_list_rgg_none_kernel(
         wb_raw = [placed([P, PACK, N // 2], F32, "wb_raw0", 18)]
         wc_w = placed([P, 2 * N], U8, "wc_w", 0)
         wa_w = placed([P, 2 * N], U8, "wa_w", 1)
-        src_runs = [(0, placed([P, EARLY], U32, "src_first", 2))]
-        dst_runs = [(0, placed([P, EARLY], U32, "dst_first", 5))]
+        src_runs = [(0, placed([P, J], U32, "src_all", 2))]
+        dst_runs = [(0, placed([P, EARLY], U32, "dst_first", 9))]
         picked = placed([P, 2 * EARLY], U8, "picked", 24)
 
         def load_scale_rows(queue, plane, rows):
@@ -217,7 +217,7 @@ def tile_list_rgg_none_kernel(
         gather(picked[:, EARLY : 2 * EARLY], tab_s, dst_list, 0, EARLY)
         move_scale_rows(nc.sync, planes[:, 0 : 2 * EARLY], picked)
         load_scale_rows(nc.sync, wa_s, wa_scales)
-        gather(src_runs[0][1][:], tab_w, src_list, 0, EARLY)
+        gather(src_runs[0][1][:], tab_w, src_list, 0, J)
         gather(dst_runs[0][1][:], tab_w, dst_list, 0, EARLY)
         quantize_wb(0)
         picked_late = placed([P, 2 * LATE], U8, "picked_late", 18.5)
@@ -231,15 +231,14 @@ def tile_list_rgg_none_kernel(
         def staged(name, width, kib):
             return placed([P, width], F32, name, kib)
 
-        make_unit(0, 0, PIECE, staged("stage_0", PIECE, 14), 0, 1, 2)
+        make_unit(0, 0, PIECE, staged("stage_0", PIECE, 17.5), 0, 1, 2)
         scatter(0, 0, PIECE)
         wb_raw.append(placed([P, PACK, N // 2], F32, "wb_raw1", 14))
         load_wb(1)
-        make_unit(1, 0, PIECE, staged("stage_1", PIECE, 54), 3, 2, 3)
-        gather_late(src_runs, src_list, "src_late", 54)
+        make_unit(1, 0, PIECE, staged("stage_1", PIECE, 21.5), 3, 2, 3)
+        gather_late(dst_runs, dst_list, "dst_late", 22)
         scatter(1, 0, PIECE)
         make_unit(0, PIECE, EARLY, staged("stage_2", LATE, 56), 2, 4, 2)
-        gather_late(dst_runs, dst_list, "dst_late", 56)
         scatter(0, PIECE, EARLY)
         make_unit(1, PIECE, EARLY, staged("stage_3", LATE, 58), 3, 4, 3)
         wb_bf.append(placed([P, 256 * PACK], BF16, "wb_bf1", 58))

@@ -40,7 +40,7 @@ def tile_list_rgg_none_kernel(
         keep = ctx.enter_context(tc.tile_pool(name="keep", bufs=1))
         psum = ctx.enter_context(tc.psum_pool(name="psum", bufs=1))
         words = ctx.enter_context(tc.tile_pool(name="words", bufs=1))
-        banks = [psum.tile([P, HALF], F32, name="bank_%d" % i) for i in range(6)]
+        banks = [psum.tile([P, HALF], F32, name="bank_%d" % i) for i in range(7)]
 
         src_list = keep.tile([P, J // LIST_ROWS], U16, name="src_list")
         dst_list = keep.tile([P, J // LIST_ROWS], U16, name="dst_list")
@@ -137,7 +137,6 @@ def tile_list_rgg_none_kernel(
         def make_unit(nt, lo, hi, stage, sums, turned, gate):
             bank_m, bank_t, bank_g = banks[sums], banks[turned], banks[gate]
             chans = slice(nt * P, (nt + 1) * P)
-            pair = slice(nt % 2 * P, (nt % 2 + 1) * P)
             blocks = [(i * P, (i + 1) * P) for i in range((hi - lo) // P)]
             for a, b in blocks:
                 nc.tensor.matmul_mx(
@@ -155,6 +154,15 @@ def tile_list_rgg_none_kernel(
             for a, b in blocks:
                 nc.tensor.transpose(bank_t[:, a:b], stage[:, a:b], ident[:])
             nc.scalar.copy(msw[nt][:, lo:hi], bank_t[:, 0 : hi - lo])
+            if (nt, lo) == (0, 0):
+                make_gate(nt, 0, P, bank_g)
+                make_gate(nt, P, hi, banks[6])
+            else:
+                make_gate(nt, lo, hi, bank_g)
+
+        def make_gate(nt, lo, hi, bank_g):
+            chans = slice(nt * P, (nt + 1) * P)
+            pair = slice(nt % 2 * P, (nt % 2 + 1) * P)
             runs = widths(lo, min(hi, EARLY)) + widths(max(lo, EARLY), hi)
             for a, b in runs:
                 nc.tensor.matmul_mx(
@@ -238,7 +246,7 @@ def tile_list_rgg_none_kernel(
         make_unit(1, 0, PIECE, staged("stage_1", PIECE, 21.5), 3, 2, 3)
         gather_late(dst_runs, dst_list, "dst_late", 22)
         scatter(1, 0, PIECE)
-        make_unit(0, PIECE, EARLY, staged("stage_2", LATE, 56), 2, 4, 2)
+        make_unit(0, PIECE, EARLY, staged("stage_2", LATE, 56), 6, 4, 6)
         scatter(0, PIECE, EARLY)
         make_unit(1, PIECE, EARLY, staged("stage_3", LATE, 58), 3, 4, 3)
         wb_bf.append(placed([P, 256 * PACK], BF16, "wb_bf1", 58))
@@ -248,7 +256,7 @@ def tile_list_rgg_none_kernel(
         make_unit(0, EARLY, J, staged("stage_4", LATE, 16), 4, 1, 4)
         scatter(0, EARLY, J)
         store(0)
-        make_unit(1, EARLY, J, staged("stage_5", LATE, 60), 2, 1, 2)
+        make_unit(1, EARLY, J, staged("stage_5", LATE, 60), 6, 1, 6)
         scatter(1, EARLY, J)
         store(1)
         stages = [keep.tile([P, HALF], F32, name="stage_wide%d" % h, align_bytes=64) for h in range(2)]

@@ -29,6 +29,7 @@ FIRST_ROW = P - SCALE_ROWS
 EARLY = 640
 LATE = J - EARLY
 PIECE = 256
+WORDS_EARLY = 768
 
 
 def tile_list_rgg_none_kernel(
@@ -40,7 +41,7 @@ def tile_list_rgg_none_kernel(
         keep = ctx.enter_context(tc.tile_pool(name="keep", bufs=1))
         psum = ctx.enter_context(tc.psum_pool(name="psum", bufs=1))
         words = ctx.enter_context(tc.tile_pool(name="words", bufs=1))
-        banks = [psum.tile([P, HALF], F32, name="bank_%d" % i) for i in range(7)]
+        banks = [psum.tile([P, HALF], F32, name="bank_%d" % i) for i in range(8)]
 
         src_list = keep.tile([P, J // LIST_ROWS], U16, name="src_list")
         dst_list = keep.tile([P, J // LIST_ROWS], U16, name="dst_list")
@@ -86,8 +87,8 @@ def tile_list_rgg_none_kernel(
         wb_raw = [placed([P, PACK, N // 2], F32, "wb_raw0", 18)]
         wc_w = placed([P, 2 * N], U8, "wc_w", 0)
         wa_w = placed([P, 2 * N], U8, "wa_w", 1)
-        src_runs = [(0, placed([P, J], U32, "src_all", 2))]
-        dst_runs = [(0, placed([P, EARLY], U32, "dst_first", 9))]
+        src_runs = [(0, placed([P, WORDS_EARLY], U32, "src_first", 2))]
+        dst_runs = [(0, placed([P, WORDS_EARLY], U32, "dst_first", 9))]
         picked = placed([P, 2 * EARLY], U8, "picked", 24)
 
         def load_scale_rows(queue, plane, rows):
@@ -121,10 +122,10 @@ def tile_list_rgg_none_kernel(
             first, run = [entry for entry in runs if entry[0] <= lo][-1]
             return run[:, lo - first : hi - first].bitcast(FP8X4)
 
-        def gather_late(runs, lst, name, kib):
-            run = placed([P, LATE], U32, name, kib)
-            runs.append((EARLY, run))
-            gather(run[:], tab_w, lst, EARLY, J)
+        def gather_late(runs, lst, lo, name, kib):
+            run = placed([P, J - lo], U32, name, kib)
+            runs.append((lo, run))
+            gather(run[:], tab_w, lst, lo, J)
 
         def widths(lo, hi):
             runs = []
@@ -138,9 +139,10 @@ def tile_list_rgg_none_kernel(
             bank_m, bank_t, bank_g = banks[sums], banks[turned], banks[gate]
             chans = slice(nt * P, (nt + 1) * P)
             blocks = [(i * P, (i + 1) * P) for i in range((hi - lo) // P)]
-            for a, b in blocks:
+            sums_of = [banks[7] if (nt, lo + a) == (0, P) else bank_m for a, b in blocks]
+            for (a, b), acc in zip(blocks, sums_of):
                 nc.tensor.matmul_mx(
-                    out=bank_m[:, a:b],
+                    out=acc[:, a:b],
                     lhsT=words_of(src_runs, lo + a, lo + b),
                     lhsT_scale=src_s(lo + a, lo + b),
                     rhs=wc_w[:, 2 * nt * P : 2 * (nt + 1) * P].bitcast(FP4X4),
@@ -148,9 +150,9 @@ def tile_list_rgg_none_kernel(
                     start=True,
                     stop=True,
                 )
-            for a, b in blocks:
+            for (a, b), acc in zip(blocks, sums_of):
                 jt = (lo + a) // P
-                nc.scalar.activation(stage[:, a:b], bank_m[:, a:b], COPY, scale=wgo_cols[:, jt : jt + 1])
+                nc.scalar.activation(stage[:, a:b], acc[:, a:b], COPY, scale=wgo_cols[:, jt : jt + 1])
             for a, b in blocks:
                 nc.tensor.transpose(bank_t[:, a:b], stage[:, a:b], ident[:])
             nc.scalar.copy(msw[nt][:, lo:hi], bank_t[:, 0 : hi - lo])
@@ -163,7 +165,7 @@ def tile_list_rgg_none_kernel(
         def make_gate(nt, lo, hi, bank_g):
             chans = slice(nt * P, (nt + 1) * P)
             pair = slice(nt % 2 * P, (nt % 2 + 1) * P)
-            runs = widths(lo, min(hi, EARLY)) + widths(max(lo, EARLY), hi)
+            runs = widths(lo, min(hi, EARLY)) + ([(EARLY, WORDS_EARLY), (WORDS_EARLY, J)] if hi == J else [])
             for a, b in runs:
                 nc.tensor.matmul_mx(
                     out=bank_g[:, a - lo : b - lo],
@@ -225,8 +227,8 @@ def tile_list_rgg_none_kernel(
         gather(picked[:, EARLY : 2 * EARLY], tab_s, dst_list, 0, EARLY)
         move_scale_rows(nc.sync, planes[:, 0 : 2 * EARLY], picked)
         load_scale_rows(nc.sync, wa_s, wa_scales)
-        gather(src_runs[0][1][:], tab_w, src_list, 0, J)
-        gather(dst_runs[0][1][:], tab_w, dst_list, 0, EARLY)
+        gather(src_runs[0][1][:], tab_w, src_list, 0, WORDS_EARLY)
+        gather(dst_runs[0][1][:], tab_w, dst_list, 0, WORDS_EARLY)
         quantize_wb(0)
         picked_late = placed([P, 2 * LATE], U8, "picked_late", 18.5)
         gather(picked_late[:, 0:LATE], tab_s, src_list, EARLY, J)
@@ -244,9 +246,10 @@ def tile_list_rgg_none_kernel(
         wb_raw.append(placed([P, PACK, N // 2], F32, "wb_raw1", 14))
         load_wb(1)
         make_unit(1, 0, PIECE, staged("stage_1", PIECE, 21.5), 3, 2, 3)
-        gather_late(dst_runs, dst_list, "dst_late", 22)
+        gather_late(src_runs, src_list, WORDS_EARLY, "src_late", 22)
         scatter(1, 0, PIECE)
         make_unit(0, PIECE, EARLY, staged("stage_2", LATE, 56), 6, 4, 6)
+        gather_late(dst_runs, dst_list, WORDS_EARLY, "dst_late", 56)
         scatter(0, PIECE, EARLY)
         make_unit(1, PIECE, EARLY, staged("stage_3", LATE, 58), 3, 4, 3)
         wb_bf.append(placed([P, 256 * PACK], BF16, "wb_bf1", 58))

@@ -29,7 +29,8 @@ FIRST_ROW = P - SCALE_ROWS
 EARLY = 640
 LATE = J - EARLY
 PIECE = 256
-WORDS_EARLY = 768
+SRC_EARLY = J - P
+DST_EARLY = J - 2 * P
 
 
 def tile_list_rgg_none_kernel(
@@ -87,8 +88,8 @@ def tile_list_rgg_none_kernel(
         wb_raw = [placed([P, PACK, N // 2], F32, "wb_raw0", 18)]
         wc_w = placed([P, 2 * N], U8, "wc_w", 0)
         wa_w = placed([P, 2 * N], U8, "wa_w", 1)
-        src_runs = [(0, placed([P, WORDS_EARLY], U32, "src_first", 2))]
-        dst_runs = [(0, placed([P, WORDS_EARLY], U32, "dst_first", 9))]
+        src_runs = [(0, placed([P, SRC_EARLY], U32, "src_first", 2))]
+        dst_runs = [(0, placed([P, DST_EARLY], U32, "dst_first", 9))]
         picked = placed([P, 2 * EARLY], U8, "picked", 24)
 
         def load_scale_rows(queue, plane, rows):
@@ -123,9 +124,9 @@ def tile_list_rgg_none_kernel(
             return run[:, lo - first : hi - first].bitcast(FP8X4)
 
         def gather_late(runs, lst, lo, name, kib):
-            run = placed([P, J - lo], U32, name, kib)
+            run = placed([P, P], U32, name, kib)
             runs.append((lo, run))
-            gather(run[:], tab_w, lst, lo, J)
+            gather(run[:], tab_w, lst, lo, lo + P)
 
         def widths(lo, hi):
             runs = []
@@ -165,7 +166,7 @@ def tile_list_rgg_none_kernel(
         def make_gate(nt, lo, hi, bank_g):
             chans = slice(nt * P, (nt + 1) * P)
             pair = slice(nt % 2 * P, (nt % 2 + 1) * P)
-            runs = widths(lo, min(hi, EARLY)) + ([(EARLY, WORDS_EARLY), (WORDS_EARLY, J)] if hi == J else [])
+            runs = widths(lo, min(hi, EARLY)) + ([(a, a + P) for a in range(EARLY, J, P)] if hi == J else [])
             for a, b in runs:
                 nc.tensor.matmul_mx(
                     out=bank_g[:, a - lo : b - lo],
@@ -176,6 +177,7 @@ def tile_list_rgg_none_kernel(
                     start=a == lo,
                     stop=False,
                 )
+            runs = widths(lo, min(hi, EARLY)) + widths(max(lo, EARLY), hi)
             for a, b in runs:
                 nc.tensor.matmul_mx(
                     out=bank_g[:, a - lo : b - lo],
@@ -227,8 +229,8 @@ def tile_list_rgg_none_kernel(
         gather(picked[:, EARLY : 2 * EARLY], tab_s, dst_list, 0, EARLY)
         move_scale_rows(nc.sync, planes[:, 0 : 2 * EARLY], picked)
         load_scale_rows(nc.sync, wa_s, wa_scales)
-        gather(src_runs[0][1][:], tab_w, src_list, 0, WORDS_EARLY)
-        gather(dst_runs[0][1][:], tab_w, dst_list, 0, WORDS_EARLY)
+        gather(src_runs[0][1][:], tab_w, src_list, 0, SRC_EARLY)
+        gather(dst_runs[0][1][:], tab_w, dst_list, 0, DST_EARLY)
         quantize_wb(0)
         picked_late = placed([P, 2 * LATE], U8, "picked_late", 18.5)
         gather(picked_late[:, 0:LATE], tab_s, src_list, EARLY, J)
@@ -246,20 +248,21 @@ def tile_list_rgg_none_kernel(
         wb_raw.append(placed([P, PACK, N // 2], F32, "wb_raw1", 14))
         load_wb(1)
         make_unit(1, 0, PIECE, staged("stage_1", PIECE, 21.5), 3, 2, 3)
-        gather_late(src_runs, src_list, WORDS_EARLY, "src_late", 22)
+        gather_late(src_runs, src_list, SRC_EARLY, "src_late", 22)
         scatter(1, 0, PIECE)
-        make_unit(0, PIECE, EARLY, staged("stage_2", LATE, 56), 6, 4, 6)
-        gather_late(dst_runs, dst_list, WORDS_EARLY, "dst_late", 56)
+        make_unit(0, PIECE, EARLY, staged("stage_2", LATE, 56), 6, 4, 2)
+        gather_late(dst_runs, dst_list, DST_EARLY, "dst_late0", 56)
         scatter(0, PIECE, EARLY)
         make_unit(1, PIECE, EARLY, staged("stage_3", LATE, 58), 3, 4, 3)
-        wb_bf.append(placed([P, 256 * PACK], BF16, "wb_bf1", 58))
+        gather_late(dst_runs, dst_list, DST_EARLY + P, "dst_late1", 57.75)
+        wb_bf.append(placed([P, 256 * PACK], BF16, "wb_bf1", 59))
         round_wb(1)
         quantize_wb(1)
         scatter(1, PIECE, EARLY)
         make_unit(0, EARLY, J, staged("stage_4", LATE, 16), 4, 1, 4)
         scatter(0, EARLY, J)
         store(0)
-        make_unit(1, EARLY, J, staged("stage_5", LATE, 60), 6, 1, 6)
+        make_unit(1, EARLY, J, staged("stage_5", LATE, 62), 2, 1, 2)
         scatter(1, EARLY, J)
         store(1)
         stages = [keep.tile([P, HALF], F32, name="stage_wide%d" % h, align_bytes=64) for h in range(2)]

@@ -29,7 +29,7 @@ FIRST_ROW = P - SCALE_ROWS
 EARLY = 640
 LATE = J - EARLY
 PIECE = 256
-SRC_EARLY = J - P
+SRC_EARLY = J - 2 * P
 DST_EARLY = J - 2 * P
 
 
@@ -123,10 +123,10 @@ def tile_list_rgg_none_kernel(
             first, run = [entry for entry in runs if entry[0] <= lo][-1]
             return run[:, lo - first : hi - first].bitcast(FP8X4)
 
-        def gather_late(runs, lst, lo, name, kib):
-            run = placed([P, P], U32, name, kib)
+        def gather_late(runs, lst, lo, hi, name, kib):
+            run = placed([P, hi - lo], U32, name, kib)
             runs.append((lo, run))
-            gather(run[:], tab_w, lst, lo, lo + P)
+            gather(run[:], tab_w, lst, lo, hi)
 
         def widths(lo, hi):
             runs = []
@@ -177,7 +177,7 @@ def tile_list_rgg_none_kernel(
                     start=a == lo,
                     stop=False,
                 )
-            runs = widths(lo, min(hi, EARLY)) + widths(max(lo, EARLY), hi)
+            runs = widths(lo, min(hi, EARLY)) + ([(EARLY, SRC_EARLY), (SRC_EARLY, J)] if hi == J else [])
             for a, b in runs:
                 nc.tensor.matmul_mx(
                     out=bank_g[:, a - lo : b - lo],
@@ -248,13 +248,13 @@ def tile_list_rgg_none_kernel(
         wb_raw.append(placed([P, PACK, N // 2], F32, "wb_raw1", 14))
         load_wb(1)
         make_unit(1, 0, PIECE, staged("stage_1", PIECE, 21.5), 3, 2, 3)
-        gather_late(src_runs, src_list, SRC_EARLY, "src_late", 22)
+        gather_late(src_runs, src_list, SRC_EARLY, J, "src_late", 22)
         scatter(1, 0, PIECE)
         make_unit(0, PIECE, EARLY, staged("stage_2", LATE, 56), 6, 4, 2)
-        gather_late(dst_runs, dst_list, DST_EARLY, "dst_late0", 56)
+        gather_late(dst_runs, dst_list, DST_EARLY, DST_EARLY + P, "dst_late0", 56)
         scatter(0, PIECE, EARLY)
         make_unit(1, PIECE, EARLY, staged("stage_3", LATE, 58), 3, 4, 3)
-        gather_late(dst_runs, dst_list, DST_EARLY + P, "dst_late1", 57.75)
+        gather_late(dst_runs, dst_list, DST_EARLY + P, J, "dst_late1", 57.75)
         wb_bf.append(placed([P, 256 * PACK], BF16, "wb_bf1", 59))
         round_wb(1)
         quantize_wb(1)

from contextlib import ExitStack

import concourse.mybir as mybir

K, N, T, J = 512, 512, 2048, 1024
FLOPS = 3 * 2 * K * N * J

F32 = mybir.dt.float32
BF16 = mybir.dt.bfloat16
I32 = mybir.dt.int32
U32 = mybir.dt.uint32
U16 = mybir.dt.uint16
U8 = mybir.dt.uint8
FP8X4 = mybir.dt.float8_e4m3fn_x4
FP4X4 = mybir.dt.float4_e2m1fn_x4
COPY = mybir.ActivationFunctionType.Copy
SIGMOID = mybir.ActivationFunctionType.Sigmoid
MULT = mybir.AluOpType.mult

P = 128
PACK = 4
HALF = 512
N_TILES = N // P
J_TILES = J // P
LIST_ROWS = 16
QUAD = 32
SCALE_ROWS = 16
FIRST_ROW = P - SCALE_ROWS
EARLY = 640
LATE = J - EARLY
PIECE = 256
SRC_EARLY = J - 2 * P
DST_EARLY = J - 2 * P


def tile_list_rgg_none_kernel(
    tc, tab_words, tab_scales, wa_words, wa_scales, wb, wc_words, wc_scales, wgo, offs, offs2, out
):
    nc = tc.nc

    with ExitStack() as ctx:
        keep = ctx.enter_context(tc.tile_pool(name="keep", bufs=1))
        psum = ctx.enter_context(tc.psum_pool(name="psum", bufs=1))
        words = ctx.enter_context(tc.tile_pool(name="words", bufs=1))
        banks = [psum.tile([P, HALF], F32, name="bank_%d" % i) for i in range(8)]

        src_list = keep.tile([P, J // LIST_ROWS], U16, name="src_list")
        dst_list = keep.tile([P, J // LIST_ROWS], U16, name="dst_list")
        tab_s = keep.tile([P, T], U8, name="tab_s", align_bytes=64)
        planes = keep.tile([P, 2 * J], U8, name="planes", align_bytes=64)
        wc_s = keep.tile([P, N], U8, name="wc_s", align_bytes=64)
        wb_w = [keep.tile([P, N // 2], U32, name="wb_w%d" % i, align_bytes=64) for i in range(2)]
        wb_s = [keep.tile([P, N // 2], U8, name="wb_s%d" % i, align_bytes=64) for i in range(2)]
        ident = keep.tile([P, P], F32, name="ident")
        wgo_rows = keep.tile([P, P], F32, name="wgo_rows")
        wgo_cols = keep.tile([P, J_TILES], F32, name="wgo_cols")
        msw = [keep.tile([P, J], F32, name="msw%d" % nt) for nt in range(N_TILES)]
        eta = [keep.tile([P, J], F32, name="eta%d" % nt) for nt in range(N_TILES)]
        warm_in = keep.tile([P, 1], F32, name="warm_in")
        warm = keep.tile([P, 1], F32, name="warm")

        def src_s(lo, hi):
            shift = 0 if lo < EARLY else EARLY
            return planes[:, lo + shift : hi + shift]

        def dst_s(lo, hi):
            shift = EARLY if lo < EARLY else J
            return planes[:, lo + shift : hi + shift]

        tab_w = words.tile([P, T], U32, name="tab_w", offset=0, align_bytes=64)

        nc.vector.memset(wc_s[:].bitcast(I32), 0)
        nc.vector.memset(warm_in[:], 0.0)
        nc.vector.memset(tab_s[0:FIRST_ROW].bitcast(I32), 0)
        nc.vector.memset(wgo_rows[:], 0.0)
        nc.vector.memset(planes[:].bitcast(I32), 0)
        with tc.tile_pool(name="early", bufs=1) as early:
            diag = early.tile([P, P], I32, name="diag")
            nc.gpsimd.iota(diag[:], [[1, P]], base=0, channel_multiplier=-1)
            nc.vector.tensor_scalar(ident[:], diag[:], 0.0, None, mybir.AluOpType.is_equal)

        late = ctx.enter_context(tc.tile_pool(name="late", bufs=1))

        def placed(shape, dtype, name, kib):
            return late.tile(shape, dtype, name=name, offset=int(kib * 1024), align_bytes=64)

        wb_bf = [placed([P, 256 * PACK], BF16, "wb_bf0", 44)]
        wb_raw = [placed([P, PACK, N // 2], F32, "wb_raw0", 18)]
        wc_w = placed([P, 2 * N], U8, "wc_w", 0)
        wa_w = placed([P, 2 * N], U8, "wa_w", 1)
        src_runs = [(0, placed([P, SRC_EARLY], U32, "src_first", 2))]
        dst_runs = [(0, placed([P, DST_EARLY], U32, "dst_first", 9))]
        picked = placed([P, 2 * EARLY], U8, "picked", 24)

        def load_scale_rows(queue, plane, rows):
            for q in range(4):
                queue.dma_start(plane[QUAD * q : QUAD * q + 4].bitcast(I32), rows[0, 4 * q : 4 * q + 4, :].bitcast(I32))

        def move_scale_rows(queue, plane, rows):
            for q in range(4):
                lo = FIRST_ROW + 4 * q
                queue.dma_start(plane[QUAD * q : QUAD * q + 4].bitcast(I32), rows[lo : lo + 4].bitcast(I32))

        def load_wb(i):
            nc.sync.dma_start(wb_raw[i][:], wb.rearrange("(p t) n -> p t n", t=PACK)[:, :, i * 256 : (i + 1) * 256])

        def entries(lst, lo, hi):
            return lst[:, lo // LIST_ROWS : hi // LIST_ROWS]

        def gather(dst, table, lst, lo, hi):
            nc.vector.tensor_copy(dst, table[:].indirect(entries(lst, lo, hi)))

        def round_wb(i):
            nc.scalar.copy(
                wb_bf[i][:].rearrange("p (c i t) -> p c t i", i=4, t=PACK),
                wb_raw[i][:].rearrange("p t (c i) -> p c t i", i=4),
            )

        def quantize_wb(i):
            nc.vector.quantize_mx(out=wb_w[i][:].bitcast(FP8X4), scales=wb_s[i][:], in_=wb_bf[i][:])

        def words_of(runs, lo, hi):
            first, run = [entry for entry in runs if entry[0] <= lo][-1]
            return run[:, lo - first : hi - first].bitcast(FP8X4)

        def gather_late(runs, lst, lo, hi, name, kib):
            run = placed([P, hi - lo], U32, name, kib)
            runs.append((lo, run))
            gather(run[:], tab_w, lst, lo, hi)

        def widths(lo, hi):
            runs = []
            for n in (HALF, 2 * P, P):
                if hi - lo >= n:
                    runs.append((lo, lo + n))
                    lo = lo + n
            return runs

        def make_unit(nt, lo, hi, stage, sums, turned, gate):
            bank_m, bank_t, bank_g = banks[sums], banks[turned], banks[gate]
            chans = slice(nt * P, (nt + 1) * P)
            blocks = [(i * P, (i + 1) * P) for i in range((hi - lo) // P)]
            sums_of = [banks[7] if (nt, lo + a) == (0, P) else bank_m for a, b in blocks]
            for (a, b), acc in zip(blocks, sums_of):
                nc.tensor.matmul_mx(
                    out=acc[:, a:b],
                    lhsT=words_of(src_runs, lo + a, lo + b),
                    lhsT_scale=src_s(lo + a, lo + b),
                    rhs=wc_w[:, 2 * nt * P : 2 * (nt + 1) * P].bitcast(FP4X4),
                    rhs_scale=wc_s[:, chans],
                    start=True,
                    stop=True,
                )
            for (a, b), acc in zip(blocks, sums_of):
                jt = (lo + a) // P
                nc.scalar.activation(stage[:, a:b], acc[:, a:b], COPY, scale=wgo_cols[:, jt : jt + 1])
            for a, b in blocks:
                nc.tensor.transpose(bank_t[:, a:b], stage[:, a:b], ident[:])
            nc.scalar.copy(msw[nt][:, lo:hi], bank_t[:, 0 : hi - lo])
            if (nt, lo) == (0, 0):
                make_gate(nt, 0, P, bank_g)
                make_gate(nt, P, hi, banks[6])
            else:
                make_gate(nt, lo, hi, bank_g)

        def make_gate(nt, lo, hi, bank_g):
            chans = slice(nt * P, (nt + 1) * P)
            pair = slice(nt % 2 * P, (nt % 2 + 1) * P)
            runs = widths(lo, min(hi, EARLY)) + ([(a, a + P) for a in range(EARLY, J, P)] if hi == J else [])
            for a, b in runs:
                nc.tensor.matmul_mx(
                    out=bank_g[:, a - lo : b - lo],
                    lhsT=wa_w[:, 2 * nt * P : 2 * (nt + 1) * P].bitcast(FP4X4),
                    lhsT_scale=wa_s[:, chans],
                    rhs=words_of(dst_runs, a, b),
                    rhs_scale=dst_s(a, b),
                    start=a == lo,
                    stop=False,
                )
            runs = widths(lo, min(hi, EARLY)) + ([(EARLY, SRC_EARLY), (SRC_EARLY, J)] if hi == J else [])
            for a, b in runs:
                nc.tensor.matmul_mx(
                    out=bank_g[:, a - lo : b - lo],
                    lhsT=wb_w[nt // 2][:, pair].bitcast(FP8X4),
                    lhsT_scale=wb_s[nt // 2][:, pair],
                    rhs=words_of(src_runs, a, b),
                    rhs_scale=src_s(a, b),
                    start=False,
                    stop=b == hi,
                )
            nc.scalar.activation(eta[nt][:, lo:hi], bank_g[:, 0 : hi - lo], SIGMOID)

        def scatter(nt, lo, hi):
            page = pages[nt % 3]
            nc.vector.tensor_tensor(page[:].indirect(entries(dst_list, lo, hi)), eta[nt][:, lo:hi], msw[nt][:, lo:hi], MULT)

        def store(nt):
            rows = slice(nt * P, (nt + 1) * P)
            nc.sync.dma_start(out[rows, :], pages[nt % 3][:])

        nc.sync.dma_start(tab_s[FIRST_ROW:P].bitcast(I32), tab_scales[0].bitcast(I32))
        nc.sync.dma_start(src_list[:], offs)
        nc.sync.dma_start(dst_list[:], offs2)
        nc.scalar.activation(warm[:], warm_in[:], SIGMOID)
        nc.sync.dma_start(tab_w[:].bitcast(I32), tab_words[0].rearrange("p t i -> p (t i)").bitcast(I32))
        load_scale_rows(nc.sync, wc_s, wc_scales)
        nc.sync.dma_start(wgo_rows[0:J_TILES, :], wgo[0, :].rearrange("(a b) -> a b", b=P))
        load_wb(0)
        nc.sync.dma_start(wc_w[:].bitcast(I32), wc_words[0].bitcast(I32))
        nc.sync.dma_start(wa_w[:].bitcast(I32), wa_words[0].bitcast(I32))

        pages = [placed([P, T], F32, "page0", 70)]
        nc.gpsimd.memset(pages[0][:], 0.0)
        wa_s = placed([P, N], U8, "wa_s", 8)
        nc.gpsimd.memset(wa_s[:].bitcast(I32), 0)

        nc.tensor.transpose(banks[1][:, 0:P], wgo_rows[:], ident[:])
        nc.scalar.copy(wgo_cols[:], banks[1][:, 0:J_TILES])
        nc.gpsimd.tensor_scalar(
            wb_bf[0][:].rearrange("p (c t) -> p c t", t=PACK),
            wb_raw[0][:].rearrange("p t c -> p c t"),
            1.0,
            0.0,
            MULT,
            mybir.AluOpType.add,
        )

        gather(picked[:, 0:EARLY], tab_s, src_list, 0, EARLY)
        gather(picked[:, EARLY : 2 * EARLY], tab_s, dst_list, 0, EARLY)
        move_scale_rows(nc.sync, planes[:, 0 : 2 * EARLY], picked)
        load_scale_rows(nc.sync, wa_s, wa_scales)
        gather(src_runs[0][1][:], tab_w, src_list, 0, SRC_EARLY)
        gather(dst_runs[0][1][:], tab_w, dst_list, 0, DST_EARLY)
        quantize_wb(0)
        picked_late = placed([P, 2 * LATE], U8, "picked_late", 18.5)
        gather(picked_late[:, 0:LATE], tab_s, src_list, EARLY, J)
        gather(picked_late[:, LATE : 2 * LATE], tab_s, dst_list, EARLY, J)
        move_scale_rows(nc.sync, planes[:, 2 * EARLY : 2 * J], picked_late)
        for i in (1, 2):
            pages.append(placed([P, T], F32, "page%d" % i, 29 + 8 * i))
            nc.gpsimd.memset(pages[i][:], 0.0)

        def staged(name, width, kib):
            return placed([P, width], F32, name, kib)

        make_unit(0, 0, PIECE, staged("stage_0", PIECE, 17.5), 0, 1, 2)
        scatter(0, 0, PIECE)
        wb_raw.append(placed([P, PACK, N // 2], F32, "wb_raw1", 14))
        load_wb(1)
        make_unit(1, 0, PIECE, staged("stage_1", PIECE, 21.5), 3, 2, 3)
        gather_late(src_runs, src_list, SRC_EARLY, J, "src_late", 22)
        scatter(1, 0, PIECE)
        make_unit(0, PIECE, EARLY, staged("stage_2", LATE, 56), 6, 4, 2)
        gather_late(dst_runs, dst_list, DST_EARLY, DST_EARLY + P, "dst_late0", 56)
        scatter(0, PIECE, EARLY)
        make_unit(1, PIECE, EARLY, staged("stage_3", LATE, 58), 3, 4, 3)
        gather_late(dst_runs, dst_list, DST_EARLY + P, J, "dst_late1", 57.75)
        wb_bf.append(placed([P, 256 * PACK], BF16, "wb_bf1", 59))
        round_wb(1)
        quantize_wb(1)
        scatter(1, PIECE, EARLY)
        make_unit(0, EARLY, J, staged("stage_4", LATE, 16), 4, 1, 4)
        scatter(0, EARLY, J)
        store(0)
        make_unit(1, EARLY, J, staged("stage_5", LATE, 62), 2, 1, 2)
        scatter(1, EARLY, J)
        store(1)
        stages = [keep.tile([P, HALF], F32, name="stage_wide%d" % h, align_bytes=64) for h in range(2)]
        for nt in range(2, N_TILES):
            for h in range(2):
                make_unit(nt, h * HALF, (h + 1) * HALF, stages[h], 3 + h, 5 * h, 3 + h)
            scatter(nt, 0, J)
            store(nt)
